import numpy as np
import ml_dtypes


def mxq(x, axis, fmt="e4m3"):
    dtype, down = {"e4m3": (ml_dtypes.float8_e4m3fn, 7), "e5m2": (ml_dtypes.float8_e5m2, 14)}[fmt]
    v = np.moveaxis(np.asarray(x, np.float32).astype(ml_dtypes.bfloat16).astype(np.float64), axis, -1)
    blocks = v.reshape(v.shape[:-1] + (-1, 32))
    amax = np.abs(blocks).max(-1, keepdims=True)
    byte = np.maximum(np.where(amax > 0, np.frexp(amax)[1] - 1 + 127, 0) - down, 1)
    scale = np.exp2(byte - 127.0)
    codes = (blocks / scale).astype(np.float32).astype(dtype).astype(np.float64)
    return np.moveaxis((codes * scale).reshape(v.shape), -1, axis)


WIDE = False


def mx_kscale(k):
    if not WIDE:
        return np.ones(k)
    levels = np.array([10, -10, 5, -5, 0])
    if k % 512:
        return np.exp2(np.random.permutation(np.resize(levels, k // 32))).repeat(32)
    a = np.empty((k // 512, 16))
    for p in range(k // 512):
        a[p, :8] = np.random.permutation(np.resize(levels, 8))
        for g in range(8):
            far = levels[np.abs(levels - a[p, g]) >= 10]
            a[p, g + 8] = far[np.random.randint(len(far))]
    return np.exp2(a.ravel()).repeat(32)


def f64(x):
    return np.asarray(x).astype(np.float64)


def striped(idx):
    return np.tile(idx.reshape(-1, 16).T, (8, 1)).astype(np.uint16)


def unstriped(offs):
    return offs[:16].T.reshape(-1).astype(np.int64)


E2M1 = np.array([0.0, 0.5, 1.0, 1.5, 2.0, 3.0, 4.0, 6.0, -0.0, -0.5, -1.0, -1.5, -2.0, -3.0, -4.0, -6.0])


def pack_weight(w, fmt):
    k, n = w.shape
    w = f64(np.asarray(w, np.float32).astype(ml_dtypes.bfloat16)).reshape(k // 32, 32, n)
    amax = np.abs(w).max(1)
    if fmt == "e4m3":
        byte = np.frexp(amax)[1] - 1 + 127 - 7
    else:
        mant, ex = np.frexp(amax / 6.0)
        byte = np.where(mant > 0.5, ex, ex - 1) + 127
    byte = np.clip(np.where(amax > 0, byte, 1), 1, 254)
    scaled = (w * np.exp2(127.0 - byte)[:, None, :]).reshape(k, n).astype(np.float32)
    by_word = np.ascontiguousarray(scaled.reshape(k // 512, 128, 4, n).transpose(0, 1, 3, 2))
    if fmt == "e4m3":
        words = by_word.astype(ml_dtypes.float8_e4m3fn).view(np.uint8)
    else:
        c = by_word.astype(ml_dtypes.float4_e2m1fn).view(np.uint8) & 0xF
        words = (c[..., 0::2] | (c[..., 1::2] << 4)).reshape(k // 512, 128, 2 * n)
    return np.ascontiguousarray(words), np.ascontiguousarray(byte.astype(np.uint8).reshape(k // 512, 16, n))


def unpack_weight(words, scales, fmt):
    g, _, n = scales.shape
    words = np.ascontiguousarray(words).reshape(g, 128, n, -1)
    if fmt == "e4m3":
        vals = words.view(ml_dtypes.float8_e4m3fn).astype(np.float64)
    else:
        nib = np.empty((g, 128, n, 4), np.uint8)
        nib[..., 0::2] = words & 0xF
        nib[..., 1::2] = words >> 4
        vals = E2M1[nib]
    vals = vals * np.repeat(np.exp2(scales.astype(np.float64) - 127.0), 8, axis=1)[..., None]
    return vals.transpose(0, 1, 3, 2).reshape(g * 512, n)


def gelu(v):
    return 0.5 * v * (1.0 + np.tanh(np.sqrt(2.0 / np.pi) * (v + 0.044715 * v**3)))


K, N, M, T, S = 1024, 1024, 1024, 2048, 1024

def setup_inputs():
    n = np.random.standard_normal
    s = mx_kscale(K)[:, None]
    u = mx_kscale(S)
    idx = np.random.permutation(T)[:S]
    tab_words, tab_scales = pack_weight(n((K, T)) * s / np.sqrt(K), "e4m3")
    x_words, x_scales = pack_weight(n((K, M)) / s, "e4m3")
    g = np.exp(0.3 * n(S)) * u
    wdT = n((N, T)) / np.sqrt(S)
    wdT[:, idx] /= u
    bd = 0.5 * n(N)
    return {"tab_words": tab_words, "tab_scales": tab_scales,
            "offs": striped(idx),
            "x_words": x_words, "x_scales": x_scales,
            "g": g.astype(np.float32),
            "wdT": wdT.astype(np.float32),
            "bd": bd.astype(np.float32)}

def reference(tab_words, tab_scales, offs, x_words, x_scales, g, wdT, bd):
    v = unpack_weight(tab_words, tab_scales, "e4m3")[:, unstriped(offs)]
    x = unpack_weight(x_words, x_scales, "e4m3")
    a = v.T @ x
    r = np.maximum(a, 0.0)
    h = np.square(r) * f64(g)[:, None]
    wd = f64(wdT)[:, unstriped(offs)]
    y = mxq(wd, 1, "e4m3") @ mxq(h, 0, "e4m3")
    return y + f64(bd)[:, None]

@@ -1,0 +1,241 @@
+from contextlib import ExitStack
+
+import concourse.mybir as mybir
+from concourse.masks import make_identity
+
+K, N, M, T, S = 1024, 1024, 1024, 2048, 1024
+FLOPS = 2 * K * S * M + 2 * S * N * M
+
+F32 = mybir.dt.float32
+BF16 = mybir.dt.bfloat16
+I32 = mybir.dt.int32
+U32 = mybir.dt.uint32
+U16 = mybir.dt.uint16
+U8 = mybir.dt.uint8
+FP8X4 = mybir.dt.float8_e4m3fn_x4
+ALU = mybir.AluOpType
+ACT = mybir.ActivationFunctionType
+
+P = 128
+PACK = 4
+PASS = P * PACK
+K_PASSES = K // PASS
+J_PASSES = S // PASS
+M_TILE = 512
+M_TILES = M // M_TILE
+N_TILES = N // P
+QUADS = 4
+LIST_COLS = PASS // 16
+SQRT_FLOOR = 2.0**-116
+
+
+def tile_list_sparse_relu2_ffn_kernel(tc, tab_words, tab_scales, offs, x_words, x_scales, g, wdT, bd, out):
+    nc = tc.nc
+    with ExitStack() as ctx:
+        keep = ctx.enter_context(tc.tile_pool(name="keep", bufs=1))
+        ring2 = ctx.enter_context(tc.tile_pool(name="ring2", bufs=2))
+        ring3 = ctx.enter_context(tc.tile_pool(name="ring3", bufs=3))
+        stage = ctx.enter_context(tc.tile_pool(name="stage", bufs=6))
+        up_psum = ctx.enter_context(tc.psum_pool(name="up_psum", bufs=3))
+        turn_psum = ctx.enter_context(tc.psum_pool(name="turn_psum", bufs=2))
+        down_psum = ctx.enter_context(tc.psum_pool(name="down_psum", bufs=3))
+
+        offsets = keep.tile([P, S // 16], U16, name="offsets")
+        nc.sync.dma_start(offsets[:], offs)
+
+        gain = keep.tile([P, J_PASSES, PACK], F32, name="gain")
+        nc.sync.dma_start(out=gain[:], in_=g.rearrange("(b p t) -> p b t", p=P, t=PACK))
+        bias = keep.tile([P, N_TILES], F32, name="bias")
+        nc.sync.dma_start(out=bias[:], in_=bd.rearrange("(p i) -> p i", i=N_TILES))
+        tab_plane = keep.tile([P, T // 4], I32, name="tab_plane", align_bytes=64)
+        x_plane = keep.tile([P, M // 4], I32, name="x_plane", align_bytes=64)
+        nc.vector.memset(tab_plane[:], 0)
+        nc.gpsimd.memset(x_plane[:], 0)
+
+        def load_plane(plane, scales):
+            for q in range(QUADS):
+                nc.sync.dma_start(
+                    out=plane[32 * q : 32 * q + 4 * K_PASSES, :],
+                    in_=scales[:, 4 * q : 4 * q + 4, :].bitcast(I32),
+                )
+
+        load_plane(tab_plane, tab_scales)
+        tab = [keep.tile([P, T], I32, name=f"tab{a}", align_bytes=64) for a in range(K_PASSES)]
+        for a in range(K_PASSES):
+            nc.sync.dma_start(out=tab[a][:], in_=tab_words[a].rearrange("p t i -> p (t i)").bitcast(I32))
+        x_codes = [keep.tile([P, K_PASSES, M_TILE], I32, name=f"x{mh}", align_bytes=64) for mh in range(M_TILES)]
+        x_view = x_words.rearrange("a p c i -> p a (c i)").bitcast(I32)
+        nc.sync.dma_start(out=x_codes[0][:], in_=x_view[:, :, 0:M_TILE])
+        load_plane(x_plane, x_scales)
+        wd_rows = wdT.rearrange("(p i) t -> i p t", i=N_TILES)
+        out_rows = out.rearrange("(p i) m -> i p m", i=N_TILES)
+        wd_win = [keep.tile([P, T], F32, name=f"wd_win{i}", align_bytes=64) for i in range(N_TILES)]
+        for i in range(2):
+            nc.sync.dma_start(out=wd_win[i][:], in_=wd_rows[i])
+        nc.sync.dma_start(out=x_codes[1][:], in_=x_view[:, :, M_TILE:M])
+        for i in range(2, N_TILES):
+            nc.sync.dma_start(out=wd_win[i][:], in_=wd_rows[i])
+
+        ident = keep.tile([P, P], F32, name="ident")
+        make_identity(nc, ident[:])
+
+        def picks(b):
+            return offsets[:, b * LIST_COLS : (b + 1) * LIST_COLS]
+
+        gain_flat = gain[:].rearrange("p b t -> p (b t)")
+        width = J_PASSES * PACK
+        floor = keep.tile([P, 1], F32, name="floor")
+        nc.gpsimd.memset(floor[:], SQRT_FLOOR)
+        sign16 = keep.tile([P, J_PASSES, 2, 2], BF16, name="sign16")
+        quarter = keep.tile([P, width], F32, name="quarter")
+        half_root = keep.tile([P, width], F32, name="half_root")
+        inv = keep.tile([P, width], F32, name="inv")
+        corr = keep.tile([P, width], F32, name="corr")
+        root = keep.tile([P, width], F32, name="root")
+        nc.scalar.activation(quarter[:], gain_flat, ACT.Abs, scale=0.25)
+        nc.scalar.activation(half_root[:], quarter[:], ACT.Sqrt, bias=floor[:])
+        nc.scalar.activation(sign16[:].rearrange("p b u e -> p (b u e)"), gain_flat, ACT.Sign, bias=floor[:])
+        nc.vector.reciprocal(inv[:], half_root[:])
+        nc.vector.tensor_tensor(corr[:], quarter[:], inv[:], ALU.mult)
+        nc.vector.tensor_tensor(root[:], corr[:], half_root[:], ALU.add)
+
+        v_scales, v_codes = [], []
+        for b in range(J_PASSES):
+            listed = keep.tile([P, PASS], U8, name=f"listed{b}", align_bytes=64)
+            nc.vector.tensor_copy(listed[:], tab_plane[:].bitcast(U8).indirect(picks(b)))
+            v_scale = keep.tile([P, PACK, P], U8, name=f"v_scale{b}", align_bytes=64)
+            nc.vector.tensor_copy(v_scale[:], listed[:].rearrange("k (p t) -> k t p", t=PACK))
+            v_scales.append(v_scale)
+        for b in range(J_PASSES):
+            codes = []
+            for a in range(K_PASSES):
+                v_code = keep.tile([P, PACK, P], U32, name=f"v_code{b}_{a}", align_bytes=64)
+                nc.vector.tensor_copy(v_code[:].rearrange("k t p -> k p t"), tab[a][:].bitcast(U32).indirect(picks(b)))
+                codes.append(v_code)
+            v_codes.append(codes)
+
+        x_scale = x_plane[:].bitcast(U8)
+        h16s, h_codes, h_scales = {}, {}, {}
+        pickeds, wd16s, wd_codes, wd_scales = {}, {}, {}, {}
+
+        def make_h(mh, b):
+            cols = slice(mh * M_TILE, (mh + 1) * M_TILE)
+            z = ring2.tile([P, PACK, M_TILE], F32, name="z")
+            for t in range(PACK):
+                acc = up_psum.tile([P, M_TILE], F32, name="acc")
+                for a in range(K_PASSES):
+                    nc.tensor.matmul_mx(
+                        out=acc[:],
+                        lhsT=v_codes[b][a][:, t, :].bitcast(FP8X4),
+                        lhsT_scale=v_scales[b][4 * a :, t, :],
+                        rhs=x_codes[mh][:, a, :].bitcast(FP8X4),
+                        rhs_scale=x_scale[4 * a :, cols],
+                        start=(a == 0),
+                        stop=(a == K_PASSES - 1),
+                    )
+                col = b * PACK + t
+                nc.scalar.activation(z[:, t, :], acc[:], ACT.Relu, scale=root[:, col : col + 1])
+            h16 = keep.tile([P, M_TILE, PACK], BF16, name=f"h16_{mh}_{b}", align_bytes=64)
+            nc.scalar.activation(
+                h16[:].rearrange("p (c i) t -> p c t i", i=4),
+                z[:].rearrange("p t (c i) -> p c t i", i=4),
+                ACT.Square,
+            )
+            h16s[mh, b] = h16
+
+        def quantize_h(mh, b):
+            h_code = keep.tile([P, M_TILE], U32, name=f"h_code{mh}_{b}", align_bytes=64)
+            h_scale = keep.tile([P, M_TILE], U8, name=f"h_scale{mh}_{b}", align_bytes=64)
+            nc.vector.quantize_mx(
+                out=h_code[:].bitcast(FP8X4), scales=h_scale[:], in_=h16s[mh, b][:].rearrange("p m t -> p (m t)")
+            )
+            h_codes[mh, b], h_scales[mh, b] = h_code, h_scale
+
+        def gather_wd(i, passes):
+            if i not in pickeds:
+                pickeds[i] = keep.tile([P, 2, J_PASSES * P, 2], BF16, name=f"picked{i}", align_bytes=64)
+            in_list_order = pickeds[i][:].rearrange("n u q e -> n q u e")
+            first, count = passes[0], len(passes)
+            nc.vector.tensor_copy(
+                in_list_order[:, first * P : (first + count) * P],
+                wd_win[i][:].indirect(offsets[:, first * LIST_COLS : (first + count) * LIST_COLS]),
+            )
+
+        def turn_wd(i, passes):
+            words = pickeds[i][:].rearrange("n u q e -> n u (q e)").bitcast(F32)
+            turned = turn_psum.tile([P, J_PASSES, 2, P], F32, name="turned")
+            if i not in wd16s:
+                wd16s[i] = ring3.tile([P, J_PASSES, P, 2, 2], BF16, name="wd16", align_bytes=64)
+            for b in passes:
+                for u in range(2):
+                    nc.tensor.transpose(turned[:, b, u, :], words[:, u, b * P : (b + 1) * P], ident[:])
+            for b in passes:
+                nc.vector.tensor_tensor(
+                    wd16s[i][:, b],
+                    turned[:, b].bitcast(BF16).rearrange("p u (n e) -> p n u e", e=2),
+                    sign16[:, b].unsqueeze(1).to_broadcast([P, P, 2, 2]),
+                    ALU.mult,
+                )
+
+        def quantize_wd(i, passes):
+            if i not in wd_codes:
+                wd_codes[i] = keep.tile([P, J_PASSES, P], U32, name=f"wd_code{i}", align_bytes=64)
+                wd_scales[i] = keep.tile([P, J_PASSES, P], U8, name=f"wd_scale{i}", align_bytes=64)
+            part = slice(passes[0], passes[0] + len(passes))
+            nc.vector.quantize_mx(
+                out=wd_codes[i][:, part].rearrange("p b n -> p (b n)").bitcast(FP8X4),
+                scales=wd_scales[i][:, part].rearrange("p b n -> p (b n)"),
+                in_=wd16s[i][:, part].rearrange("p b n u e -> p (b n u e)"),
+            )
+
+        def down(i, mh, on_vector=False):
+            y = down_psum.tile([P, M_TILE], F32, name="y")
+            for b in range(J_PASSES):
+                nc.tensor.matmul_mx(
+                    out=y[:],
+                    lhsT=wd_codes[i][:, b, :].bitcast(FP8X4),
+                    lhsT_scale=wd_scales[i][:, b, :],
+                    rhs=h_codes[mh, b][:].bitcast(FP8X4),
+                    rhs_scale=h_scales[mh, b][:],
+                    start=(b == 0),
+                    stop=(b == J_PASSES - 1),
+                )
+            result = stage.tile([P, M_TILE], F32, name="result")
+            if on_vector:
+                nc.vector.tensor_scalar(result[:], y[:], bias[:, i : i + 1], None, ALU.add)
+            else:
+                nc.scalar.activation(result[:], y[:], ACT.Identity, bias=bias[:, i : i + 1])
+            nc.sync.dma_start(out=out_rows[i][:, mh * M_TILE : (mh + 1) * M_TILE], in_=result[:])
+
+        both = [0, 1]
+        for mh in range(M_TILES):
+            for b in range(J_PASSES):
+                make_h(mh, b)
+        h_after = {0: (0, 0), 1: (0, 1), 3: (1, 0), 4: (1, 1)}
+        last = N_TILES - 1
+        gather_wd(0, both)
+        for i in range(last):
+            if i + 1 < last:
+                gather_wd(i + 1, both)
+            else:
+                gather_wd(last, [0])
+            turn_wd(i, both)
+            if i in h_after:
+                quantize_h(*h_after[i])
+            if i + 1 == last:
+                gather_wd(last, [1])
+            quantize_wd(i, both)
+            if i == 4:
+                for done in range(5):
+                    down(done, 0)
+                for done in range(5):
+                    down(done, 1)
+            elif i > 4:
+                down(i, 0)
+                down(i, 1)
+        turn_wd(last, [0])
+        turn_wd(last, [1])
+        quantize_wd(last, [0])
+        quantize_wd(last, [1])
+        down(last, 0)
+        down(last, 1, on_vector=True)

@@ -26,6 +26,7 @@ M_TILES = M // M_TILE
 N_TILES = N // P
 QUADS = 4
 LIST_COLS = PASS // 16
+WIN_BYTES = 4 * T
 SQRT_FLOOR = 2.0**-116
 
 
@@ -34,46 +35,47 @@ def tile_list_sparse_relu2_ffn_kernel(tc, tab_words, tab_scales, offs, x_words, 
     with ExitStack() as ctx:
         keep = ctx.enter_context(tc.tile_pool(name="keep", bufs=1))
         ring2 = ctx.enter_context(tc.tile_pool(name="ring2", bufs=2))
-        ring3 = ctx.enter_context(tc.tile_pool(name="ring3", bufs=3))
-        stage = ctx.enter_context(tc.tile_pool(name="stage", bufs=6))
-        up_psum = ctx.enter_context(tc.psum_pool(name="up_psum", bufs=3))
+        shared = ctx.enter_context(tc.tile_pool(name="shared", bufs=1))
+        stage = ctx.enter_context(tc.tile_pool(name="stage", bufs=16))
+        sum_psum = ctx.enter_context(tc.psum_pool(name="sum_psum", bufs=6))
         turn_psum = ctx.enter_context(tc.psum_pool(name="turn_psum", bufs=2))
-        down_psum = ctx.enter_context(tc.psum_pool(name="down_psum", bufs=3))
 
         offsets = keep.tile([P, S // 16], U16, name="offsets")
         nc.sync.dma_start(offsets[:], offs)
 
         gain = keep.tile([P, J_PASSES, PACK], F32, name="gain")
         nc.sync.dma_start(out=gain[:], in_=g.rearrange("(b p t) -> p b t", p=P, t=PACK))
-        bias = keep.tile([P, N_TILES], F32, name="bias")
-        nc.sync.dma_start(out=bias[:], in_=bd.rearrange("(p i) -> p i", i=N_TILES))
         tab_plane = keep.tile([P, T // 4], I32, name="tab_plane", align_bytes=64)
         x_plane = keep.tile([P, M // 4], I32, name="x_plane", align_bytes=64)
         nc.vector.memset(tab_plane[:], 0)
         nc.gpsimd.memset(x_plane[:], 0)
 
-        def load_plane(plane, scales):
+        def load_plane(queue, plane, scales):
             for q in range(QUADS):
-                nc.sync.dma_start(
+                queue.dma_start(
                     out=plane[32 * q : 32 * q + 4 * K_PASSES, :],
                     in_=scales[:, 4 * q : 4 * q + 4, :].bitcast(I32),
                 )
 
-        load_plane(tab_plane, tab_scales)
+        load_plane(nc.sync, tab_plane, tab_scales)
         tab = [keep.tile([P, T], I32, name=f"tab{a}", align_bytes=64) for a in range(K_PASSES)]
         for a in range(K_PASSES):
             nc.sync.dma_start(out=tab[a][:], in_=tab_words[a].rearrange("p t i -> p (t i)").bitcast(I32))
         x_codes = [keep.tile([P, K_PASSES, M_TILE], I32, name=f"x{mh}", align_bytes=64) for mh in range(M_TILES)]
         x_view = x_words.rearrange("a p c i -> p a (c i)").bitcast(I32)
         nc.sync.dma_start(out=x_codes[0][:], in_=x_view[:, :, 0:M_TILE])
-        load_plane(x_plane, x_scales)
+        load_plane(nc.sync, x_plane, x_scales)
         wd_rows = wdT.rearrange("(p i) t -> i p t", i=N_TILES)
         out_rows = out.rearrange("(p i) m -> i p m", i=N_TILES)
-        wd_win = [keep.tile([P, T], F32, name=f"wd_win{i}", align_bytes=64) for i in range(N_TILES)]
-        for i in range(2):
+        wd_win = [
+            shared.tile([P, T], F32, name=f"wd_win{i}", align_bytes=64, offset=i * WIN_BYTES) for i in range(N_TILES)
+        ]
+        for i in range(3):
             nc.sync.dma_start(out=wd_win[i][:], in_=wd_rows[i])
         nc.sync.dma_start(out=x_codes[1][:], in_=x_view[:, :, M_TILE:M])
-        for i in range(2, N_TILES):
+        bias = keep.tile([P, N_TILES], F32, name="bias")
+        nc.sync.dma_start(out=bias[:], in_=bd.rearrange("(p i) -> p i", i=N_TILES))
+        for i in range(3, N_TILES):
             nc.sync.dma_start(out=wd_win[i][:], in_=wd_rows[i])
 
         ident = keep.tile([P, P], F32, name="ident")
@@ -84,34 +86,34 @@ def tile_list_sparse_relu2_ffn_kernel(tc, tab_words, tab_scales, offs, x_words, 
 
         gain_flat = gain[:].rearrange("p b t -> p (b t)")
         width = J_PASSES * PACK
+        def small(name):
+            return keep.tile([P, width], F32, name=name)
+
         floor = keep.tile([P, 1], F32, name="floor")
-        nc.gpsimd.memset(floor[:], SQRT_FLOOR)
-        sign16 = keep.tile([P, J_PASSES, 2, 2], BF16, name="sign16")
-        quarter = keep.tile([P, width], F32, name="quarter")
-        half_root = keep.tile([P, width], F32, name="half_root")
-        inv = keep.tile([P, width], F32, name="inv")
-        corr = keep.tile([P, width], F32, name="corr")
-        root = keep.tile([P, width], F32, name="root")
-        nc.scalar.activation(quarter[:], gain_flat, ACT.Abs, scale=0.25)
-        nc.scalar.activation(half_root[:], quarter[:], ACT.Sqrt, bias=floor[:])
-        nc.scalar.activation(sign16[:].rearrange("p b u e -> p (b u e)"), gain_flat, ACT.Sign, bias=floor[:])
+        nc.vector.memset(floor[:], SQRT_FLOOR)
+        mag, half_root, inv, corr, root = small("mag"), small("half_root"), small("inv"), small("corr"), small("root")
+        nc.vector.scalar_tensor_tensor(mag[:], gain_flat, -1.0, gain_flat, ALU.mult, ALU.max)
+        nc.scalar.activation(half_root[:], mag[:], ACT.Sqrt, bias=floor[:], scale=0.25)
         nc.vector.reciprocal(inv[:], half_root[:])
-        nc.vector.tensor_tensor(corr[:], quarter[:], inv[:], ALU.mult)
+        nc.vector.scalar_tensor_tensor(corr[:], mag[:], 0.25, inv[:], ALU.mult, ALU.mult)
         nc.vector.tensor_tensor(root[:], corr[:], half_root[:], ALU.add)
+        twice_ge = small("twice_ge")
+        sign16 = keep.tile([P, J_PASSES, 2, 2], BF16, name="sign16")
+        nc.gpsimd.tensor_scalar(twice_ge[:], gain_flat, 0.0, 2.0, ALU.is_ge, ALU.mult)
+        nc.gpsimd.tensor_scalar(
+            sign16[:].rearrange("p b u e -> p (b u e)"), twice_ge[:], 1.0, -1.0, ALU.mult, ALU.add
+        )
 
         v_scales, v_codes = [], []
         for b in range(J_PASSES):
+            codes = [keep.tile([P, PACK, P], U32, name=f"v_code{b}_{a}", align_bytes=64) for a in range(K_PASSES)]
             listed = keep.tile([P, PASS], U8, name=f"listed{b}", align_bytes=64)
-            nc.vector.tensor_copy(listed[:], tab_plane[:].bitcast(U8).indirect(picks(b)))
             v_scale = keep.tile([P, PACK, P], U8, name=f"v_scale{b}", align_bytes=64)
+            nc.vector.tensor_copy(codes[0][:].rearrange("k t p -> k p t"), tab[0][:].bitcast(U32).indirect(picks(b)))
+            nc.vector.tensor_copy(listed[:], tab_plane[:].bitcast(U8).indirect(picks(b)))
+            nc.vector.tensor_copy(codes[1][:].rearrange("k t p -> k p t"), tab[1][:].bitcast(U32).indirect(picks(b)))
             nc.vector.tensor_copy(v_scale[:], listed[:].rearrange("k (p t) -> k t p", t=PACK))
             v_scales.append(v_scale)
-        for b in range(J_PASSES):
-            codes = []
-            for a in range(K_PASSES):
-                v_code = keep.tile([P, PACK, P], U32, name=f"v_code{b}_{a}", align_bytes=64)
-                nc.vector.tensor_copy(v_code[:].rearrange("k t p -> k p t"), tab[a][:].bitcast(U32).indirect(picks(b)))
-                codes.append(v_code)
             v_codes.append(codes)
 
         x_scale = x_plane[:].bitcast(U8)
@@ -122,7 +124,7 @@ def tile_list_sparse_relu2_ffn_kernel(tc, tab_words, tab_scales, offs, x_words, 
             cols = slice(mh * M_TILE, (mh + 1) * M_TILE)
             z = ring2.tile([P, PACK, M_TILE], F32, name="z")
             for t in range(PACK):
-                acc = up_psum.tile([P, M_TILE], F32, name="acc")
+                acc = sum_psum.tile([P, M_TILE], F32, name="acc")
                 for a in range(K_PASSES):
                     nc.tensor.matmul_mx(
                         out=acc[:],
@@ -163,23 +165,33 @@ def tile_list_sparse_relu2_ffn_kernel(tc, tab_words, tab_scales, offs, x_words, 
 
         def turn_wd(i, passes):
             words = pickeds[i][:].rearrange("n u q e -> n u (q e)").bitcast(F32)
-            turned = turn_psum.tile([P, J_PASSES, 2, P], F32, name="turned")
+            turned = turn_psum.tile([P, 2, J_PASSES, P], F32, name="turned")
             if i not in wd16s:
-                wd16s[i] = ring3.tile([P, J_PASSES, P, 2, 2], BF16, name="wd16", align_bytes=64)
+                if i < N_TILES - 1:
+                    wd16s[i] = shared.tile(
+                        [P, J_PASSES, P, 2, 2], BF16, name=f"wd16_{i}", align_bytes=64, offset=(i + 1) * WIN_BYTES
+                    )
+                else:
+                    wd16s[i] = keep.tile([P, J_PASSES, P, 2, 2], BF16, name=f"wd16_{i}", align_bytes=64)
             for b in passes:
                 for u in range(2):
-                    nc.tensor.transpose(turned[:, b, u, :], words[:, u, b * P : (b + 1) * P], ident[:])
-            for b in passes:
-                nc.vector.tensor_tensor(
-                    wd16s[i][:, b],
-                    turned[:, b].bitcast(BF16).rearrange("p u (n e) -> p n u e", e=2),
-                    sign16[:, b].unsqueeze(1).to_broadcast([P, P, 2, 2]),
-                    ALU.mult,
-                )
+                    nc.tensor.transpose(turned[:, u, b, :], words[:, u, b * P : (b + 1) * P], ident[:])
+            part = slice(passes[0], passes[0] + len(passes))
+            nc.vector.tensor_tensor(
+                wd16s[i][:, part],
+                turned[:, :, part].bitcast(BF16).rearrange("p u b (n e) -> p b n u e", e=2),
+                sign16[:, part].unsqueeze(2).to_broadcast([P, len(passes), P, 2, 2]),
+                ALU.mult,
+            )
 
         def quantize_wd(i, passes):
             if i not in wd_codes:
-                wd_codes[i] = keep.tile([P, J_PASSES, P], U32, name=f"wd_code{i}", align_bytes=64)
+                if i < N_TILES - 3:
+                    wd_codes[i] = shared.tile(
+                        [P, J_PASSES, P], U32, name=f"wd_code{i}", align_bytes=64, offset=(i + 2) * WIN_BYTES + 2 * S
+                    )
+                else:
+                    wd_codes[i] = keep.tile([P, J_PASSES, P], U32, name=f"wd_code{i}", align_bytes=64)
                 wd_scales[i] = keep.tile([P, J_PASSES, P], U8, name=f"wd_scale{i}", align_bytes=64)
             part = slice(passes[0], passes[0] + len(passes))
             nc.vector.quantize_mx(
@@ -189,7 +201,7 @@ def tile_list_sparse_relu2_ffn_kernel(tc, tab_words, tab_scales, offs, x_words, 
             )
 
         def down(i, mh, on_vector=False):
-            y = down_psum.tile([P, M_TILE], F32, name="y")
+            y = sum_psum.tile([P, M_TILE], F32, name="acc")
             for b in range(J_PASSES):
                 nc.tensor.matmul_mx(
                     out=y[:],
@@ -211,7 +223,7 @@ def tile_list_sparse_relu2_ffn_kernel(tc, tab_words, tab_scales, offs, x_words, 
         for mh in range(M_TILES):
             for b in range(J_PASSES):
                 make_h(mh, b)
-        h_after = {0: (0, 0), 1: (0, 1), 3: (1, 0), 4: (1, 1)}
+        h_after = {1: (0, 0), 2: (0, 1), 3: (1, 0), 4: (1, 1)}
         last = N_TILES - 1
         gather_wd(0, both)
         for i in range(last):
@@ -219,23 +231,19 @@ def tile_list_sparse_relu2_ffn_kernel(tc, tab_words, tab_scales, offs, x_words, 
                 gather_wd(i + 1, both)
             else:
                 gather_wd(last, [0])
+                gather_wd(last, [1])
+            if 1 <= i <= last - 2:
+                quantize_wd(i - 1, both)
             turn_wd(i, both)
             if i in h_after:
                 quantize_h(*h_after[i])
-            if i + 1 == last:
-                gather_wd(last, [1])
-            quantize_wd(i, both)
-            if i == 4:
-                for done in range(5):
-                    down(done, 0)
-                for done in range(5):
-                    down(done, 1)
-            elif i > 4:
-                down(i, 0)
-                down(i, 1)
+            if i == last - 2:
+                quantize_wd(i, both)
         turn_wd(last, [0])
+        quantize_wd(last - 1, both)
         turn_wd(last, [1])
         quantize_wd(last, [0])
         quantize_wd(last, [1])
-        down(last, 0)
-        down(last, 1, on_vector=True)
+        for i in range(N_TILES):
+            down(i, 0)
+            down(i, 1, on_vector=(i >= last - 1))

@@ -28,6 +28,10 @@ QUADS = 4
 LIST_COLS = PASS // 16
 WIN_BYTES = 4 * T
 SQRT_FLOOR = 2.0**-116
+DIRECT = 4
+PAIRED = (2, 3)
+LOAD_COLS = 1024
+CAST_COLS = 512
 
 
 def tile_list_sparse_relu2_ffn_kernel(tc, tab_words, tab_scales, offs, x_words, x_scales, g, wdT, bd, out):
@@ -65,18 +69,25 @@ def tile_list_sparse_relu2_ffn_kernel(tc, tab_words, tab_scales, offs, x_words, 
         x_view = x_words.rearrange("a p c i -> p a (c i)").bitcast(I32)
         nc.sync.dma_start(out=x_codes[0][:], in_=x_view[:, :, 0:M_TILE])
         load_plane(nc.sync, x_plane, x_scales)
-        wd_rows = wdT.rearrange("(p i) t -> i p t", i=N_TILES)
+        wd_rows = wdT.rearrange("(p i) t -> p i t", i=N_TILES)
         out_rows = out.rearrange("(p i) m -> i p m", i=N_TILES)
         wd_win = [
-            shared.tile([P, T], F32, name=f"wd_win{i}", align_bytes=64, offset=i * WIN_BYTES) for i in range(N_TILES)
+            shared.tile([P, T], F32, name=f"wd_win{i}", align_bytes=64, offset=i * WIN_BYTES) for i in range(DIRECT)
         ]
         for i in range(3):
-            nc.sync.dma_start(out=wd_win[i][:], in_=wd_rows[i])
+            nc.sync.dma_start(out=wd_win[i][:], in_=wd_rows[:, i])
         nc.sync.dma_start(out=x_codes[1][:], in_=x_view[:, :, M_TILE:M])
         bias = keep.tile([P, N_TILES], F32, name="bias")
         nc.sync.dma_start(out=bias[:], in_=bd.rearrange("(p i) -> p i", i=N_TILES))
-        for i in range(3, N_TILES):
-            nc.sync.dma_start(out=wd_win[i][:], in_=wd_rows[i])
+        for i in range(3, DIRECT):
+            nc.sync.dma_start(out=wd_win[i][:], in_=wd_rows[:, i])
+        raw = {}
+        for d in PAIRED:
+            for c in range(T // LOAD_COLS):
+                raw[d, c] = keep.tile([P, 2, LOAD_COLS], F32, name=f"raw{d}_{c}", align_bytes=64)
+                nc.sync.dma_start(
+                    out=raw[d, c][:], in_=wd_rows[:, 2 * d : 2 * d + 2, c * LOAD_COLS : (c + 1) * LOAD_COLS]
+                )
 
         ident = keep.tile([P, P], F32, name="ident")
         make_identity(nc, ident[:])
@@ -137,67 +148,96 @@ def tile_list_sparse_relu2_ffn_kernel(tc, tab_words, tab_scales, offs, x_words, 
                     )
                 col = b * PACK + t
                 nc.scalar.activation(z[:, t, :], acc[:], ACT.Relu, scale=root[:, col : col + 1])
-            h16 = keep.tile([P, M_TILE, PACK], BF16, name=f"h16_{mh}_{b}", align_bytes=64)
+            if mh not in h16s:
+                h16s[mh] = keep.tile([P, J_PASSES, M_TILE, PACK], BF16, name=f"h16_{mh}", align_bytes=64)
             nc.scalar.activation(
-                h16[:].rearrange("p (c i) t -> p c t i", i=4),
+                h16s[mh][:, b].rearrange("p (c i) t -> p c t i", i=4),
                 z[:].rearrange("p t (c i) -> p c t i", i=4),
                 ACT.Square,
             )
-            h16s[mh, b] = h16
 
-        def quantize_h(mh, b):
-            h_code = keep.tile([P, M_TILE], U32, name=f"h_code{mh}_{b}", align_bytes=64)
-            h_scale = keep.tile([P, M_TILE], U8, name=f"h_scale{mh}_{b}", align_bytes=64)
+        def quantize_h(mh, offset=None):
+            h_code = keep.tile([P, J_PASSES, M_TILE], U32, name=f"h_code{mh}", align_bytes=64)
+            if offset is None:
+                h_scale = keep.tile([P, J_PASSES, M_TILE], U8, name=f"h_scale{mh}", align_bytes=64)
+            else:
+                h_scale = shared.tile([P, J_PASSES, M_TILE], U8, name=f"h_scale{mh}", align_bytes=64, offset=offset)
             nc.vector.quantize_mx(
-                out=h_code[:].bitcast(FP8X4), scales=h_scale[:], in_=h16s[mh, b][:].rearrange("p m t -> p (m t)")
+                out=h_code[:].rearrange("p b m -> p (b m)").bitcast(FP8X4),
+                scales=h_scale[:].rearrange("p b m -> p (b m)"),
+                in_=h16s[mh][:].rearrange("p b m t -> p (b m t)"),
             )
-            h_codes[mh, b], h_scales[mh, b] = h_code, h_scale
+            h_codes[mh], h_scales[mh] = h_code, h_scale
 
-        def gather_wd(i, passes):
-            if i not in pickeds:
-                pickeds[i] = keep.tile([P, 2, J_PASSES * P, 2], BF16, name=f"picked{i}", align_bytes=64)
-            in_list_order = pickeds[i][:].rearrange("n u q e -> n q u e")
-            first, count = passes[0], len(passes)
-            nc.vector.tensor_copy(
-                in_list_order[:, first * P : (first + count) * P],
-                wd_win[i][:].indirect(offsets[:, first * LIST_COLS : (first + count) * LIST_COLS]),
-            )
+        def gather_wd(i):
+            pickeds[i] = keep.tile([P, 2, J_PASSES * P, 2], BF16, name=f"picked{i}", align_bytes=64)
+            nc.vector.tensor_copy(pickeds[i][:].rearrange("n u q e -> n q u e"), wd_win[i][:].indirect(offsets[:]))
 
-        def turn_wd(i, passes):
+        def duo_tile(d, offset=None):
+            if offset is None:
+                wd16s[d] = keep.tile([P, 2, J_PASSES, P, PACK], BF16, name=f"wd16_{d}", align_bytes=64)
+            else:
+                wd16s[d] = shared.tile([P, 2, J_PASSES, P, PACK], BF16, name=f"wd16_{d}", align_bytes=64, offset=offset)
+
+        def turn_wd(i):
             words = pickeds[i][:].rearrange("n u q e -> n u (q e)").bitcast(F32)
             turned = turn_psum.tile([P, 2, J_PASSES, P], F32, name="turned")
-            if i not in wd16s:
-                if i < N_TILES - 1:
-                    wd16s[i] = shared.tile(
-                        [P, J_PASSES, P, 2, 2], BF16, name=f"wd16_{i}", align_bytes=64, offset=(i + 1) * WIN_BYTES
-                    )
-                else:
-                    wd16s[i] = keep.tile([P, J_PASSES, P, 2, 2], BF16, name=f"wd16_{i}", align_bytes=64)
-            for b in passes:
+            for b in range(J_PASSES):
                 for u in range(2):
                     nc.tensor.transpose(turned[:, u, b, :], words[:, u, b * P : (b + 1) * P], ident[:])
-            part = slice(passes[0], passes[0] + len(passes))
             nc.vector.tensor_tensor(
-                wd16s[i][:, part],
-                turned[:, :, part].bitcast(BF16).rearrange("p u b (n e) -> p b n u e", e=2),
-                sign16[:, part].unsqueeze(2).to_broadcast([P, len(passes), P, 2, 2]),
+                wd16s[i // 2][:, i % 2].rearrange("p b n (u e) -> p b n u e", e=2),
+                turned[:].bitcast(BF16).rearrange("p u b (n e) -> p b n u e", e=2),
+                sign16[:].unsqueeze(2).to_broadcast([P, J_PASSES, P, 2, 2]),
                 ALU.mult,
             )
 
-        def quantize_wd(i, passes):
-            if i not in wd_codes:
-                if i < N_TILES - 3:
-                    wd_codes[i] = shared.tile(
-                        [P, J_PASSES, P], U32, name=f"wd_code{i}", align_bytes=64, offset=(i + 2) * WIN_BYTES + 2 * S
-                    )
+        pair_wins, banks = {}, {}
+
+        def cast_pair(d):
+            pair_wins[d] = shared.tile(
+                [P, T, 2], BF16, name=f"pair_win{d}", align_bytes=64, offset=(DIRECT + d - 2) * WIN_BYTES
+            )
+            for c0 in range(0, T, CAST_COLS):
+                c, lo = divmod(c0, LOAD_COLS)
+                nc.gpsimd.tensor_copy(
+                    pair_wins[d][:, c0 : c0 + CAST_COLS, :],
+                    raw[d, c][:, :, lo : lo + CAST_COLS].rearrange("p e t -> p t e"),
+                )
+
+        def gather_pair(d, b):
+            picked = keep.tile([P, PACK, P], U32, name=f"pair_picked{d}_{b}", align_bytes=64)
+            window = pair_wins[d][:].rearrange("p t e -> p (t e)").bitcast(U32)
+            nc.vector.tensor_copy(picked[:].rearrange("n t q -> n q t"), window.indirect(picks(b)))
+            turned = turn_psum.tile([P, 2, J_PASSES, P], F32, name="turned")
+            bank = turned[:].rearrange("q u v n -> q (u v) n")
+            for t in range(PACK):
+                nc.tensor.transpose(bank[:, t, :], picked[:, t, :].bitcast(F32), ident[:])
+            banks[d, b] = bank
+
+        def part_pair(d, b, halves):
+            signs = sign16[:, b].rearrange("p u e -> p (u e)")
+            count = halves.stop - halves.start
+            nc.vector.tensor_tensor(
+                wd16s[d][:, halves, b],
+                banks[d, b].bitcast(BF16).rearrange("q t (n e) -> q e n t", e=2)[:, halves],
+                signs.unsqueeze(1).unsqueeze(1).to_broadcast([P, count, P, PACK]),
+                ALU.mult,
+            )
+
+        def quantize_wd(d, halves, offset=None):
+            if d not in wd_codes:
+                wd_codes[d] = keep.tile([P, 2, J_PASSES, P], U32, name=f"wd_code{d}", align_bytes=64)
+                if offset is None:
+                    wd_scales[d] = keep.tile([P, 2, J_PASSES, P], U8, name=f"wd_scale{d}", align_bytes=64)
                 else:
-                    wd_codes[i] = keep.tile([P, J_PASSES, P], U32, name=f"wd_code{i}", align_bytes=64)
-                wd_scales[i] = keep.tile([P, J_PASSES, P], U8, name=f"wd_scale{i}", align_bytes=64)
-            part = slice(passes[0], passes[0] + len(passes))
+                    wd_scales[d] = shared.tile(
+                        [P, 2, J_PASSES, P], U8, name=f"wd_scale{d}", align_bytes=64, offset=offset
+                    )
             nc.vector.quantize_mx(
-                out=wd_codes[i][:, part].rearrange("p b n -> p (b n)").bitcast(FP8X4),
-                scales=wd_scales[i][:, part].rearrange("p b n -> p (b n)"),
-                in_=wd16s[i][:, part].rearrange("p b n u e -> p (b n u e)"),
+                out=wd_codes[d][:, halves].rearrange("p e b n -> p (e b n)").bitcast(FP8X4),
+                scales=wd_scales[d][:, halves].rearrange("p e b n -> p (e b n)"),
+                in_=wd16s[d][:, halves].rearrange("p e b n t -> p (e b n t)"),
             )
 
         def down(i, mh, on_vector=False):
@@ -205,10 +245,10 @@ def tile_list_sparse_relu2_ffn_kernel(tc, tab_words, tab_scales, offs, x_words, 
             for b in range(J_PASSES):
                 nc.tensor.matmul_mx(
                     out=y[:],
-                    lhsT=wd_codes[i][:, b, :].bitcast(FP8X4),
-                    lhsT_scale=wd_scales[i][:, b, :],
-                    rhs=h_codes[mh, b][:].bitcast(FP8X4),
-                    rhs_scale=h_scales[mh, b][:],
+                    lhsT=wd_codes[i // 2][:, i % 2, b, :].bitcast(FP8X4),
+                    lhsT_scale=wd_scales[i // 2][:, i % 2, b, :],
+                    rhs=h_codes[mh][:, b].bitcast(FP8X4),
+                    rhs_scale=h_scales[mh][:, b],
                     start=(b == 0),
                     stop=(b == J_PASSES - 1),
                 )
@@ -219,31 +259,47 @@ def tile_list_sparse_relu2_ffn_kernel(tc, tab_words, tab_scales, offs, x_words, 
                 nc.scalar.activation(result[:], y[:], ACT.Identity, bias=bias[:, i : i + 1])
             nc.sync.dma_start(out=out_rows[i][:, mh * M_TILE : (mh + 1) * M_TILE], in_=result[:])
 
-        both = [0, 1]
+        both, first, second = slice(0, 2), slice(0, 1), slice(1, 2)
         for mh in range(M_TILES):
             for b in range(J_PASSES):
                 make_h(mh, b)
-        h_after = {1: (0, 0), 2: (0, 1), 3: (1, 0), 4: (1, 1)}
-        last = N_TILES - 1
-        gather_wd(0, both)
-        for i in range(last):
-            if i + 1 < last:
-                gather_wd(i + 1, both)
-            else:
-                gather_wd(last, [0])
-                gather_wd(last, [1])
-            if 1 <= i <= last - 2:
-                quantize_wd(i - 1, both)
-            turn_wd(i, both)
-            if i in h_after:
-                quantize_h(*h_after[i])
-            if i == last - 2:
-                quantize_wd(i, both)
-        turn_wd(last, [0])
-        quantize_wd(last - 1, both)
-        turn_wd(last, [1])
-        quantize_wd(last, [0])
-        quantize_wd(last, [1])
-        for i in range(N_TILES):
+        for d in PAIRED:
+            cast_pair(d)
+        duo_tile(0, 2 * WIN_BYTES)
+        duo_tile(1, 3 * WIN_BYTES)
+        duo_tile(2)
+        duo_tile(3)
+        for i in range(3):
+            gather_wd(i)
+        turn_wd(0)
+        turn_wd(1)
+        gather_wd(3)
+        turn_wd(2)
+        quantize_wd(0, both, 3 * WIN_BYTES + 4096)
+        turn_wd(3)
+        quantize_h(0, 3 * WIN_BYTES + 5120)
+        quantize_wd(1, both)
+        for i in range(DIRECT):
             down(i, 0)
-            down(i, 1, on_vector=(i >= last - 1))
+        gather_pair(2, 0)
+        gather_pair(2, 1)
+        part_pair(2, 0, both)
+        part_pair(2, 1, both)
+        quantize_h(1, DIRECT * WIN_BYTES)
+        quantize_wd(2, both)
+        for i in range(DIRECT):
+            down(i, 1)
+        gather_pair(3, 0)
+        gather_pair(3, 1)
+        for i in range(DIRECT, DIRECT + 2):
+            down(i, 0)
+            down(i, 1)
+        part_pair(3, 0, both)
+        part_pair(3, 1, first)
+        quantize_wd(3, first)
+        part_pair(3, 1, second)
+        quantize_wd(3, second)
+        down(6, 0)
+        down(6, 1)
+        down(7, 0, on_vector=True)
+        down(7, 1)

@@ -32,15 +32,16 @@ DIRECT = 4
 PAIRED = (2, 3)
 LOAD_COLS = 1024
 CAST_COLS = 512
+TAB_AT = 6 * WIN_BYTES
+Z_AT = 7 * WIN_BYTES
 
 
 def tile_list_sparse_relu2_ffn_kernel(tc, tab_words, tab_scales, offs, x_words, x_scales, g, wdT, bd, out):
     nc = tc.nc
     with ExitStack() as ctx:
         keep = ctx.enter_context(tc.tile_pool(name="keep", bufs=1))
-        ring2 = ctx.enter_context(tc.tile_pool(name="ring2", bufs=2))
         shared = ctx.enter_context(tc.tile_pool(name="shared", bufs=1))
-        stage = ctx.enter_context(tc.tile_pool(name="stage", bufs=16))
+        stage = ctx.enter_context(tc.tile_pool(name="stage", bufs=12))
         sum_psum = ctx.enter_context(tc.psum_pool(name="sum_psum", bufs=6))
         turn_psum = ctx.enter_context(tc.psum_pool(name="turn_psum", bufs=2))
 
@@ -62,7 +63,10 @@ def tile_list_sparse_relu2_ffn_kernel(tc, tab_words, tab_scales, offs, x_words, 
                 )
 
         load_plane(nc.sync, tab_plane, tab_scales)
-        tab = [keep.tile([P, T], I32, name=f"tab{a}", align_bytes=64) for a in range(K_PASSES)]
+        tab = [
+            keep.tile([P, T], I32, name="tab0", align_bytes=64),
+            shared.tile([P, T], I32, name="tab1", align_bytes=64, offset=TAB_AT),
+        ]
         for a in range(K_PASSES):
             nc.sync.dma_start(out=tab[a][:], in_=tab_words[a].rearrange("p t i -> p (t i)").bitcast(I32))
         x_codes = [keep.tile([P, K_PASSES, M_TILE], I32, name=f"x{mh}", align_bytes=64) for mh in range(M_TILES)]
@@ -74,20 +78,26 @@ def tile_list_sparse_relu2_ffn_kernel(tc, tab_words, tab_scales, offs, x_words, 
         wd_win = [
             shared.tile([P, T], F32, name=f"wd_win{i}", align_bytes=64, offset=i * WIN_BYTES) for i in range(DIRECT)
         ]
-        for i in range(3):
+        raw = {}
+
+        def load_row_tile(i):
             nc.sync.dma_start(out=wd_win[i][:], in_=wd_rows[:, i])
+
+        def load_pair_part(d, c):
+            raw[d, c] = keep.tile([P, 2, LOAD_COLS], F32, name=f"raw{d}_{c}", align_bytes=64)
+            nc.sync.dma_start(out=raw[d, c][:], in_=wd_rows[:, 2 * d : 2 * d + 2, c * LOAD_COLS : (c + 1) * LOAD_COLS])
+
+        load_row_tile(0)
+        load_row_tile(1)
+        load_pair_part(2, 0)
         nc.sync.dma_start(out=x_codes[1][:], in_=x_view[:, :, M_TILE:M])
         bias = keep.tile([P, N_TILES], F32, name="bias")
         nc.sync.dma_start(out=bias[:], in_=bd.rearrange("(p i) -> p i", i=N_TILES))
-        for i in range(3, DIRECT):
-            nc.sync.dma_start(out=wd_win[i][:], in_=wd_rows[:, i])
-        raw = {}
-        for d in PAIRED:
-            for c in range(T // LOAD_COLS):
-                raw[d, c] = keep.tile([P, 2, LOAD_COLS], F32, name=f"raw{d}_{c}", align_bytes=64)
-                nc.sync.dma_start(
-                    out=raw[d, c][:], in_=wd_rows[:, 2 * d : 2 * d + 2, c * LOAD_COLS : (c + 1) * LOAD_COLS]
-                )
+        load_row_tile(2)
+        load_pair_part(2, 1)
+        load_row_tile(3)
+        load_pair_part(3, 0)
+        load_pair_part(3, 1)
 
         ident = keep.tile([P, P], F32, name="ident")
         make_identity(nc, ident[:])
@@ -115,17 +125,24 @@ def tile_list_sparse_relu2_ffn_kernel(tc, tab_words, tab_scales, offs, x_words, 
             sign16[:].rearrange("p b u e -> p (b u e)"), twice_ge[:], 1.0, -1.0, ALU.mult, ALU.add
         )
 
-        v_scales, v_codes = [], []
-        for b in range(J_PASSES):
-            codes = [keep.tile([P, PACK, P], U32, name=f"v_code{b}_{a}", align_bytes=64) for a in range(K_PASSES)]
-            listed = keep.tile([P, PASS], U8, name=f"listed{b}", align_bytes=64)
-            v_scale = keep.tile([P, PACK, P], U8, name=f"v_scale{b}", align_bytes=64)
-            nc.vector.tensor_copy(codes[0][:].rearrange("k t p -> k p t"), tab[0][:].bitcast(U32).indirect(picks(b)))
-            nc.vector.tensor_copy(listed[:], tab_plane[:].bitcast(U8).indirect(picks(b)))
-            nc.vector.tensor_copy(codes[1][:].rearrange("k t p -> k p t"), tab[1][:].bitcast(U32).indirect(picks(b)))
-            nc.vector.tensor_copy(v_scale[:], listed[:].rearrange("k (p t) -> k t p", t=PACK))
-            v_scales.append(v_scale)
-            v_codes.append(codes)
+        listed = keep.tile([P, S], U8, name="listed", align_bytes=64)
+        v_scale = keep.tile([P, J_PASSES, PACK, P], U8, name="v_scale", align_bytes=64)
+        nc.vector.tensor_copy(listed[:], tab_plane[:].bitcast(U8).indirect(offsets[:]))
+        v_codes = {}
+
+        def gather_table(b, a, offset=None):
+            if offset is None:
+                codes = keep.tile([P, PACK, P], U32, name=f"v_code{b}_{a}", align_bytes=64)
+            else:
+                codes = shared.tile([P, PACK, P], U32, name=f"v_code{b}_{a}", align_bytes=64, offset=offset)
+            nc.vector.tensor_copy(codes[:].rearrange("k t p -> k p t"), tab[a][:].bitcast(U32).indirect(picks(b)))
+            v_codes[b, a] = codes
+
+        gather_table(0, 0)
+        nc.vector.tensor_copy(v_scale[:], listed[:].rearrange("k (b p t) -> k b t p", b=J_PASSES, t=PACK))
+        gather_table(0, 1)
+        gather_table(1, 1)
+        gather_table(1, 0, TAB_AT)
 
         x_scale = x_plane[:].bitcast(U8)
         h16s, h_codes, h_scales = {}, {}, {}
@@ -133,14 +150,14 @@ def tile_list_sparse_relu2_ffn_kernel(tc, tab_words, tab_scales, offs, x_words, 
 
         def make_h(mh, b):
             cols = slice(mh * M_TILE, (mh + 1) * M_TILE)
-            z = ring2.tile([P, PACK, M_TILE], F32, name="z")
+            z = shared.tile([P, PACK, M_TILE], F32, name=f"z{mh}_{b}", align_bytes=64, offset=Z_AT + b * WIN_BYTES)
             for t in range(PACK):
                 acc = sum_psum.tile([P, M_TILE], F32, name="acc")
                 for a in range(K_PASSES):
                     nc.tensor.matmul_mx(
                         out=acc[:],
-                        lhsT=v_codes[b][a][:, t, :].bitcast(FP8X4),
-                        lhsT_scale=v_scales[b][4 * a :, t, :],
+                        lhsT=v_codes[b, a][:, t, :].bitcast(FP8X4),
+                        lhsT_scale=v_scale[4 * a :, b, t, :],
                         rhs=x_codes[mh][:, a, :].bitcast(FP8X4),
                         rhs_scale=x_scale[4 * a :, cols],
                         start=(a == 0),
@@ -156,18 +173,20 @@ def tile_list_sparse_relu2_ffn_kernel(tc, tab_words, tab_scales, offs, x_words, 
                 ACT.Square,
             )
 
-        def quantize_h(mh, offset=None):
-            h_code = keep.tile([P, J_PASSES, M_TILE], U32, name=f"h_code{mh}", align_bytes=64)
-            if offset is None:
-                h_scale = keep.tile([P, J_PASSES, M_TILE], U8, name=f"h_scale{mh}", align_bytes=64)
-            else:
-                h_scale = shared.tile([P, J_PASSES, M_TILE], U8, name=f"h_scale{mh}", align_bytes=64, offset=offset)
-            nc.vector.quantize_mx(
-                out=h_code[:].rearrange("p b m -> p (b m)").bitcast(FP8X4),
-                scales=h_scale[:].rearrange("p b m -> p (b m)"),
-                in_=h16s[mh][:].rearrange("p b m t -> p (b m t)"),
+        def quantize_h(mh, passes, offset):
+            if mh not in h_codes:
+                h_codes[mh] = keep.tile([P, J_PASSES, M_TILE], U32, name=f"h_code{mh}", align_bytes=64)
+            count = passes.stop - passes.start
+            h_scale = shared.tile(
+                [P, count, M_TILE], U8, name=f"h_scale{mh}_{passes.start}", align_bytes=64, offset=offset
             )
-            h_codes[mh], h_scales[mh] = h_code, h_scale
+            nc.vector.quantize_mx(
+                out=h_codes[mh][:, passes].rearrange("p b m -> p (b m)").bitcast(FP8X4),
+                scales=h_scale[:].rearrange("p b m -> p (b m)"),
+                in_=h16s[mh][:, passes].rearrange("p b m t -> p (b m t)"),
+            )
+            for b in range(count):
+                h_scales[mh, passes.start + b] = h_scale[:, b]
 
         def gather_wd(i):
             pickeds[i] = keep.tile([P, 2, J_PASSES * P, 2], BF16, name=f"picked{i}", align_bytes=64)
@@ -201,12 +220,15 @@ def tile_list_sparse_relu2_ffn_kernel(tc, tab_words, tab_scales, offs, x_words, 
             for c0 in range(0, T, CAST_COLS):
                 c, lo = divmod(c0, LOAD_COLS)
                 nc.gpsimd.tensor_copy(
-                    pair_wins[d][:, c0 : c0 + CAST_COLS, :],
-                    raw[d, c][:, :, lo : lo + CAST_COLS].rearrange("p e t -> p t e"),
+                    pair_wins[d][:, c0 : c0 + CAST_COLS, :].rearrange("p (c i) e -> p c e i", i=4),
+                    raw[d, c][:, :, lo : lo + CAST_COLS].rearrange("p e (c i) -> p c e i", i=4),
                 )
 
-        def gather_pair(d, b):
-            picked = keep.tile([P, PACK, P], U32, name=f"pair_picked{d}_{b}", align_bytes=64)
+        def gather_pair(d, b, offset=None):
+            if offset is None:
+                picked = keep.tile([P, PACK, P], U32, name=f"pair_picked{d}_{b}", align_bytes=64)
+            else:
+                picked = shared.tile([P, PACK, P], U32, name=f"pair_picked{d}_{b}", align_bytes=64, offset=offset)
             window = pair_wins[d][:].rearrange("p t e -> p (t e)").bitcast(U32)
             nc.vector.tensor_copy(picked[:].rearrange("n t q -> n q t"), window.indirect(picks(b)))
             turned = turn_psum.tile([P, 2, J_PASSES, P], F32, name="turned")
@@ -248,11 +270,16 @@ def tile_list_sparse_relu2_ffn_kernel(tc, tab_words, tab_scales, offs, x_words, 
                     lhsT=wd_codes[i // 2][:, i % 2, b, :].bitcast(FP8X4),
                     lhsT_scale=wd_scales[i // 2][:, i % 2, b, :],
                     rhs=h_codes[mh][:, b].bitcast(FP8X4),
-                    rhs_scale=h_scales[mh][:, b],
+                    rhs_scale=h_scales[mh, b],
                     start=(b == 0),
                     stop=(b == J_PASSES - 1),
                 )
-            result = stage.tile([P, M_TILE], F32, name="result")
+            if mh == 0 and i < DIRECT:
+                result = shared.tile(
+                    [P, M_TILE], F32, name=f"result{i}", align_bytes=64, offset=Z_AT + WIN_BYTES + i * 4 * M_TILE
+                )
+            else:
+                result = stage.tile([P, M_TILE], F32, name="result")
             if on_vector:
                 nc.vector.tensor_scalar(result[:], y[:], bias[:, i : i + 1], None, ALU.add)
             else:
@@ -265,32 +292,34 @@ def tile_list_sparse_relu2_ffn_kernel(tc, tab_words, tab_scales, offs, x_words, 
                 make_h(mh, b)
         for d in PAIRED:
             cast_pair(d)
-        duo_tile(0, 2 * WIN_BYTES)
-        duo_tile(1, 3 * WIN_BYTES)
+        duo_tile(0, WIN_BYTES)
+        duo_tile(1)
         duo_tile(2)
         duo_tile(3)
-        for i in range(3):
-            gather_wd(i)
+        gather_wd(0)
+        gather_wd(1)
         turn_wd(0)
         turn_wd(1)
-        gather_wd(3)
+        quantize_wd(0, both)
+        gather_wd(2)
+        quantize_h(0, both, 2 * WIN_BYTES)
         turn_wd(2)
-        quantize_wd(0, both, 3 * WIN_BYTES + 4096)
+        gather_wd(3)
+        quantize_h(1, first, 3 * WIN_BYTES + 4096)
         turn_wd(3)
-        quantize_h(0, 3 * WIN_BYTES + 5120)
+        gather_pair(2, 0, 3 * WIN_BYTES)
         quantize_wd(1, both)
+        gather_pair(2, 1, 3 * WIN_BYTES + 2048)
         for i in range(DIRECT):
             down(i, 0)
-        gather_pair(2, 0)
-        gather_pair(2, 1)
-        part_pair(2, 0, both)
-        part_pair(2, 1, both)
-        quantize_h(1, DIRECT * WIN_BYTES)
-        quantize_wd(2, both)
+        quantize_h(1, second, DIRECT * WIN_BYTES)
         for i in range(DIRECT):
             down(i, 1)
+        part_pair(2, 0, both)
+        part_pair(2, 1, both)
         gather_pair(3, 0)
         gather_pair(3, 1)
+        quantize_wd(2, both, (DIRECT + 1) * WIN_BYTES)
         for i in range(DIRECT, DIRECT + 2):
             down(i, 0)
             down(i, 1)

@@ -206,8 +206,8 @@ def tile_list_sparse_relu2_ffn_kernel(tc, tab_words, tab_scales, offs, x_words, 
                     nc.tensor.transpose(turned[:, u, b, :], words[:, u, b * P : (b + 1) * P], ident[:])
             nc.vector.tensor_tensor(
                 wd16s[i // 2][:, i % 2].rearrange("p b n (u e) -> p b n u e", e=2),
-                turned[:].bitcast(BF16).rearrange("p u b (n e) -> p b n u e", e=2),
                 sign16[:].unsqueeze(2).to_broadcast([P, J_PASSES, P, 2, 2]),
+                turned[:].bitcast(BF16).rearrange("p u b (n e) -> p b n u e", e=2),
                 ALU.mult,
             )
 
@@ -242,8 +242,8 @@ def tile_list_sparse_relu2_ffn_kernel(tc, tab_words, tab_scales, offs, x_words, 
             count = halves.stop - halves.start
             nc.vector.tensor_tensor(
                 wd16s[d][:, halves, b],
-                banks[d, b].bitcast(BF16).rearrange("q t (n e) -> q e n t", e=2)[:, halves],
                 signs.unsqueeze(1).unsqueeze(1).to_broadcast([P, count, P, PACK]),
+                banks[d, b].bitcast(BF16).rearrange("q t (n e) -> q e n t", e=2)[:, halves],
                 ALU.mult,
             )
 

@@ -28,12 +28,18 @@ QUADS = 4
 LIST_COLS = PASS // 16
 WIN_BYTES = 4 * T
 SQRT_FLOOR = 2.0**-116
-DIRECT = 4
-PAIRED = (2, 3)
+SINGLES = 4
+COUPLES = (2, 3)
 LOAD_COLS = 1024
 CAST_COLS = 512
-TAB_AT = 6 * WIN_BYTES
-Z_AT = 7 * WIN_BYTES
+COUPLE_AT = SINGLES * WIN_BYTES
+BANK_BYTES = 2048
+RING = 6
+Z_AT = COUPLE_AT + len(COUPLES) * WIN_BYTES
+H_AT = Z_AT + J_PASSES * WIN_BYTES
+LAST_H_AT = H_AT + WIN_BYTES + WIN_BYTES // 2
+RAW_AT = H_AT + M_TILES * WIN_BYTES
+PICKED_AT = RAW_AT + 4 * WIN_BYTES
 
 
 def tile_list_sparse_relu2_ffn_kernel(tc, tab_words, tab_scales, offs, x_words, x_scales, g, wdT, bd, out):
@@ -42,62 +48,70 @@ def tile_list_sparse_relu2_ffn_kernel(tc, tab_words, tab_scales, offs, x_words, 
         keep = ctx.enter_context(tc.tile_pool(name="keep", bufs=1))
         shared = ctx.enter_context(tc.tile_pool(name="shared", bufs=1))
         stage = ctx.enter_context(tc.tile_pool(name="stage", bufs=12))
-        sum_psum = ctx.enter_context(tc.psum_pool(name="sum_psum", bufs=6))
-        turn_psum = ctx.enter_context(tc.psum_pool(name="turn_psum", bufs=2))
+        psum = ctx.enter_context(tc.psum_pool(name="psum", bufs=1))
+
+        def place(shape, dtype, name, offset=None):
+            if offset is None:
+                return keep.tile(shape, dtype, name=name, align_bytes=64)
+            return shared.tile(shape, dtype, name=name, align_bytes=64, offset=offset)
+
+        def bank_tile(shape, name, bank):
+            return psum.tile(shape, F32, name=name, offset=bank * BANK_BYTES)
 
         offsets = keep.tile([P, S // 16], U16, name="offsets")
         nc.sync.dma_start(offsets[:], offs)
 
         gain = keep.tile([P, J_PASSES, PACK], F32, name="gain")
         nc.sync.dma_start(out=gain[:], in_=g.rearrange("(b p t) -> p b t", p=P, t=PACK))
-        tab_plane = keep.tile([P, T // 4], I32, name="tab_plane", align_bytes=64)
-        x_plane = keep.tile([P, M // 4], I32, name="x_plane", align_bytes=64)
-        nc.vector.memset(tab_plane[:], 0)
-        nc.gpsimd.memset(x_plane[:], 0)
-
-        def load_plane(queue, plane, scales):
-            for q in range(QUADS):
-                queue.dma_start(
-                    out=plane[32 * q : 32 * q + 4 * K_PASSES, :],
-                    in_=scales[:, 4 * q : 4 * q + 4, :].bitcast(I32),
-                )
-
-        load_plane(nc.sync, tab_plane, tab_scales)
-        tab = [
-            keep.tile([P, T], I32, name="tab0", align_bytes=64),
-            shared.tile([P, T], I32, name="tab1", align_bytes=64, offset=TAB_AT),
-        ]
-        for a in range(K_PASSES):
-            nc.sync.dma_start(out=tab[a][:], in_=tab_words[a].rearrange("p t i -> p (t i)").bitcast(I32))
-        x_codes = [keep.tile([P, K_PASSES, M_TILE], I32, name=f"x{mh}", align_bytes=64) for mh in range(M_TILES)]
+        tab_plane = place([P, T], U8, "tab_plane")
+        x_plane = place([P, K_PASSES, M], U8, "x_plane")
+        nc.gpsimd.memset(tab_plane[:].bitcast(I32), 0)
+        nc.gpsimd.memset(x_plane[:].bitcast(I32), 0)
+        for q in range(QUADS):
+            nc.sync.dma_start(
+                out=tab_plane[32 * q : 32 * q + 4 * K_PASSES, :].bitcast(I32),
+                in_=tab_scales[:, 4 * q : 4 * q + 4, :].bitcast(I32),
+            )
+        tab = [place([P, T], I32, f"tab{a}") for a in range(K_PASSES)]
         x_view = x_words.rearrange("a p c i -> p a (c i)").bitcast(I32)
-        nc.sync.dma_start(out=x_codes[0][:], in_=x_view[:, :, 0:M_TILE])
-        load_plane(nc.sync, x_plane, x_scales)
+        x_first = [place([P, M_TILE], I32, f"x_first{a}") for a in range(K_PASSES)]
+        x_second = place([P, K_PASSES, M_TILE], I32, "x_second")
+
+        def load_table(a):
+            nc.sync.dma_start(out=tab[a][:], in_=tab_words[a].rearrange("p t i -> p (t i)").bitcast(I32))
+            nc.sync.dma_start(out=x_first[a][:], in_=x_view[:, a, 0:M_TILE])
+
+        load_table(0)
+        for q in range(QUADS):
+            nc.sync.dma_start(
+                out=x_plane[32 * q : 32 * q + 4].bitcast(I32),
+                in_=x_scales[:, 4 * q : 4 * q + 4, :].rearrange("a r c -> r a c").bitcast(I32),
+            )
+        load_table(1)
+
         wd_rows = wdT.rearrange("(p i) t -> p i t", i=N_TILES)
         out_rows = out.rearrange("(p i) m -> i p m", i=N_TILES)
-        wd_win = [
-            shared.tile([P, T], F32, name=f"wd_win{i}", align_bytes=64, offset=i * WIN_BYTES) for i in range(DIRECT)
-        ]
+        wd_win = [place([P, T], F32, f"wd_win{i}", i * WIN_BYTES) for i in range(SINGLES)]
         raw = {}
 
-        def load_row_tile(i):
+        def load_single(i):
             nc.sync.dma_start(out=wd_win[i][:], in_=wd_rows[:, i])
 
-        def load_pair_part(d, c):
-            raw[d, c] = keep.tile([P, 2, LOAD_COLS], F32, name=f"raw{d}_{c}", align_bytes=64)
+        def load_couple_part(d, c):
+            raw[d, c] = place([P, 2, LOAD_COLS], F32, f"raw{d}_{c}", RAW_AT + (2 * (d - 2) + c) * WIN_BYTES)
             nc.sync.dma_start(out=raw[d, c][:], in_=wd_rows[:, 2 * d : 2 * d + 2, c * LOAD_COLS : (c + 1) * LOAD_COLS])
 
-        load_row_tile(0)
-        load_row_tile(1)
-        load_pair_part(2, 0)
-        nc.sync.dma_start(out=x_codes[1][:], in_=x_view[:, :, M_TILE:M])
+        load_single(0)
+        load_single(1)
+        load_couple_part(2, 0)
+        nc.sync.dma_start(out=x_second[:], in_=x_view[:, :, M_TILE:M])
         bias = keep.tile([P, N_TILES], F32, name="bias")
         nc.sync.dma_start(out=bias[:], in_=bd.rearrange("(p i) -> p i", i=N_TILES))
-        load_row_tile(2)
-        load_pair_part(2, 1)
-        load_row_tile(3)
-        load_pair_part(3, 0)
-        load_pair_part(3, 1)
+        load_single(2)
+        load_couple_part(2, 1)
+        load_couple_part(3, 0)
+        load_single(3)
+        load_couple_part(3, 1)
 
         ident = keep.tile([P, P], F32, name="ident")
         make_identity(nc, ident[:])
@@ -107,79 +121,70 @@ def tile_list_sparse_relu2_ffn_kernel(tc, tab_words, tab_scales, offs, x_words, 
 
         gain_flat = gain[:].rearrange("p b t -> p (b t)")
         width = J_PASSES * PACK
-        def small(name):
-            return keep.tile([P, width], F32, name=name)
-
         floor = keep.tile([P, 1], F32, name="floor")
-        nc.vector.memset(floor[:], SQRT_FLOOR)
-        mag, half_root, inv, corr, root = small("mag"), small("half_root"), small("inv"), small("corr"), small("root")
-        nc.vector.scalar_tensor_tensor(mag[:], gain_flat, -1.0, gain_flat, ALU.mult, ALU.max)
-        nc.scalar.activation(half_root[:], mag[:], ACT.Sqrt, bias=floor[:], scale=0.25)
-        nc.vector.reciprocal(inv[:], half_root[:])
-        nc.vector.scalar_tensor_tensor(corr[:], mag[:], 0.25, inv[:], ALU.mult, ALU.mult)
-        nc.vector.tensor_tensor(root[:], corr[:], half_root[:], ALU.add)
-        twice_ge = small("twice_ge")
-        sign16 = keep.tile([P, J_PASSES, 2, 2], BF16, name="sign16")
+        nc.gpsimd.memset(floor[:], SQRT_FLOOR)
+        mag = keep.tile([P, width], F32, name="mag")
+        root = keep.tile([P, width], F32, name="root")
+        twice_ge = keep.tile([P, width], F32, name="twice_ge")
+        sign16 = keep.tile([P, J_PASSES, PACK], BF16, name="sign16")
+        sign_flat = sign16[:].rearrange("p b t -> p (b t)")
         nc.gpsimd.tensor_scalar(twice_ge[:], gain_flat, 0.0, 2.0, ALU.is_ge, ALU.mult)
-        nc.gpsimd.tensor_scalar(
-            sign16[:].rearrange("p b u e -> p (b u e)"), twice_ge[:], 1.0, -1.0, ALU.mult, ALU.add
-        )
+        nc.gpsimd.tensor_scalar(sign_flat, twice_ge[:], 1.0, -1.0, ALU.mult, ALU.add)
+        nc.gpsimd.tensor_tensor(mag[:], gain_flat, sign_flat, ALU.mult)
+        nc.scalar.activation(root[:], mag[:], ACT.Sqrt, bias=floor[:])
 
-        listed = keep.tile([P, S], U8, name="listed", align_bytes=64)
-        v_scale = keep.tile([P, J_PASSES, PACK, P], U8, name="v_scale", align_bytes=64)
-        nc.vector.tensor_copy(listed[:], tab_plane[:].bitcast(U8).indirect(offsets[:]))
+        v_scale = place([P, J_PASSES, PACK, P], U8, "v_scale")
+        nc.vector.tensor_copy(v_scale[:].rearrange("k b t p -> k b p t"), tab_plane[:].indirect(offsets[:]))
         v_codes = {}
+        for a in range(K_PASSES):
+            for b in range(J_PASSES):
+                v_codes[b, a] = place([P, PACK, P], U32, f"v_code{b}_{a}")
+                nc.vector.tensor_copy(
+                    v_codes[b, a][:].rearrange("k t p -> k p t"), tab[a][:].bitcast(U32).indirect(picks(b))
+                )
 
-        def gather_table(b, a, offset=None):
-            if offset is None:
-                codes = keep.tile([P, PACK, P], U32, name=f"v_code{b}_{a}", align_bytes=64)
-            else:
-                codes = shared.tile([P, PACK, P], U32, name=f"v_code{b}_{a}", align_bytes=64, offset=offset)
-            nc.vector.tensor_copy(codes[:].rearrange("k t p -> k p t"), tab[a][:].bitcast(U32).indirect(picks(b)))
-            v_codes[b, a] = codes
-
-        gather_table(0, 0)
-        nc.vector.tensor_copy(v_scale[:], listed[:].rearrange("k (b p t) -> k b t p", b=J_PASSES, t=PACK))
-        gather_table(0, 1)
-        gather_table(1, 1)
-        gather_table(1, 0, TAB_AT)
-
-        x_scale = x_plane[:].bitcast(U8)
         h16s, h_codes, h_scales = {}, {}, {}
         pickeds, wd16s, wd_codes, wd_scales = {}, {}, {}, {}
 
+        def up_pass(acc, mh, b, t, a):
+            x_codes = x_first[a][:] if mh == 0 else x_second[:, a, :]
+            nc.tensor.matmul_mx(
+                out=acc[:],
+                lhsT=v_codes[b, a][:, t, :].bitcast(FP8X4),
+                lhsT_scale=v_scale[4 * a :, b, t, :],
+                rhs=x_codes.bitcast(FP8X4),
+                rhs_scale=x_plane[:, a, mh * M_TILE : (mh + 1) * M_TILE],
+                start=(a == 0),
+                stop=(a == K_PASSES - 1),
+            )
+
         def make_h(mh, b):
-            cols = slice(mh * M_TILE, (mh + 1) * M_TILE)
-            z = shared.tile([P, PACK, M_TILE], F32, name=f"z{mh}_{b}", align_bytes=64, offset=Z_AT + b * WIN_BYTES)
+            z = place([P, PACK, M_TILE], F32, f"z{mh}_{b}", Z_AT + b * WIN_BYTES)
+            group = (mh * J_PASSES + b) * PACK
+            accs = [bank_tile([P, M_TILE], f"up{group + t}", (group + t) % RING) for t in range(PACK)]
+            if group == 0:
+                for t in range(PACK):
+                    up_pass(accs[t], mh, b, t, 0)
             for t in range(PACK):
-                acc = sum_psum.tile([P, M_TILE], F32, name="acc")
-                for a in range(K_PASSES):
-                    nc.tensor.matmul_mx(
-                        out=acc[:],
-                        lhsT=v_codes[b, a][:, t, :].bitcast(FP8X4),
-                        lhsT_scale=v_scale[4 * a :, b, t, :],
-                        rhs=x_codes[mh][:, a, :].bitcast(FP8X4),
-                        rhs_scale=x_scale[4 * a :, cols],
-                        start=(a == 0),
-                        stop=(a == K_PASSES - 1),
-                    )
+                acc = accs[t]
+                if group > 0:
+                    up_pass(acc, mh, b, t, 0)
+                up_pass(acc, mh, b, t, 1)
                 col = b * PACK + t
                 nc.scalar.activation(z[:, t, :], acc[:], ACT.Relu, scale=root[:, col : col + 1])
             if mh not in h16s:
-                h16s[mh] = keep.tile([P, J_PASSES, M_TILE, PACK], BF16, name=f"h16_{mh}", align_bytes=64)
+                h16s[mh] = place([P, J_PASSES, M_TILE, PACK], BF16, f"h16_{mh}", H_AT + mh * WIN_BYTES)
             nc.scalar.activation(
                 h16s[mh][:, b].rearrange("p (c i) t -> p c t i", i=4),
                 z[:].rearrange("p t (c i) -> p c t i", i=4),
                 ACT.Square,
             )
 
-        def quantize_h(mh, passes, offset):
+        def quantize_h(mh, passes, offset=None):
             if mh not in h_codes:
-                h_codes[mh] = keep.tile([P, J_PASSES, M_TILE], U32, name=f"h_code{mh}", align_bytes=64)
+                h_codes[mh] = place([P, J_PASSES, M_TILE], U32, f"h_code{mh}")
             count = passes.stop - passes.start
-            h_scale = shared.tile(
-                [P, count, M_TILE], U8, name=f"h_scale{mh}_{passes.start}", align_bytes=64, offset=offset
-            )
+            h_scale = place([P, count, M_TILE], U8, f"h_scale{mh}_{passes.start}", offset)
             nc.vector.quantize_mx(
                 out=h_codes[mh][:, passes].rearrange("p b m -> p (b m)").bitcast(FP8X4),
                 scales=h_scale[:].rearrange("p b m -> p (b m)"),
@@ -188,98 +193,87 @@ def tile_list_sparse_relu2_ffn_kernel(tc, tab_words, tab_scales, offs, x_words, 
             for b in range(count):
                 h_scales[mh, passes.start + b] = h_scale[:, b]
 
-        def gather_wd(i):
-            pickeds[i] = keep.tile([P, 2, J_PASSES * P, 2], BF16, name=f"picked{i}", align_bytes=64)
+        def gather_single(i, offset=None):
+            pickeds[i] = place([P, 2, J_PASSES * P, 2], BF16, f"picked{i}", offset)
             nc.vector.tensor_copy(pickeds[i][:].rearrange("n u q e -> n q u e"), wd_win[i][:].indirect(offsets[:]))
 
-        def duo_tile(d, offset=None):
-            if offset is None:
-                wd16s[d] = keep.tile([P, 2, J_PASSES, P, PACK], BF16, name=f"wd16_{d}", align_bytes=64)
-            else:
-                wd16s[d] = shared.tile([P, 2, J_PASSES, P, PACK], BF16, name=f"wd16_{d}", align_bytes=64, offset=offset)
+        def rounded_tile(first_tile, count, offset=None):
+            tile = place([P, count, J_PASSES, P, PACK], BF16, f"wd16_{first_tile}", offset)
+            for e in range(count):
+                wd16s[first_tile + e] = (tile, e)
 
-        def turn_wd(i):
+        def turn_single(i, bank):
             words = pickeds[i][:].rearrange("n u q e -> n u (q e)").bitcast(F32)
-            turned = turn_psum.tile([P, 2, J_PASSES, P], F32, name="turned")
+            turned = bank_tile([P, 2, J_PASSES, P], f"turned{i}", bank)
             for b in range(J_PASSES):
                 for u in range(2):
                     nc.tensor.transpose(turned[:, u, b, :], words[:, u, b * P : (b + 1) * P], ident[:])
+            tile, e = wd16s[i]
+            signs = sign16[:].rearrange("p b (u e) -> p b u e", e=2)
             nc.vector.tensor_tensor(
-                wd16s[i // 2][:, i % 2].rearrange("p b n (u e) -> p b n u e", e=2),
-                sign16[:].unsqueeze(2).to_broadcast([P, J_PASSES, P, 2, 2]),
+                tile[:, e].rearrange("p b n (u e) -> p b n u e", e=2),
+                signs.unsqueeze(2).to_broadcast([P, J_PASSES, P, 2, 2]),
                 turned[:].bitcast(BF16).rearrange("p u b (n e) -> p b n u e", e=2),
                 ALU.mult,
             )
 
-        pair_wins, banks = {}, {}
+        couple_wins, banks = {}, {}
 
-        def cast_pair(d):
-            pair_wins[d] = shared.tile(
-                [P, T, 2], BF16, name=f"pair_win{d}", align_bytes=64, offset=(DIRECT + d - 2) * WIN_BYTES
-            )
+        def cast_couple(d):
+            couple_wins[d] = place([P, T, 2], BF16, f"couple_win{d}", COUPLE_AT + (d - 2) * WIN_BYTES)
             for c0 in range(0, T, CAST_COLS):
                 c, lo = divmod(c0, LOAD_COLS)
                 nc.gpsimd.tensor_copy(
-                    pair_wins[d][:, c0 : c0 + CAST_COLS, :].rearrange("p (c i) e -> p c e i", i=4),
+                    couple_wins[d][:, c0 : c0 + CAST_COLS, :].rearrange("p (c i) e -> p c e i", i=4),
                     raw[d, c][:, :, lo : lo + CAST_COLS].rearrange("p e (c i) -> p c e i", i=4),
                 )
 
-        def gather_pair(d, b, offset=None):
-            if offset is None:
-                picked = keep.tile([P, PACK, P], U32, name=f"pair_picked{d}_{b}", align_bytes=64)
-            else:
-                picked = shared.tile([P, PACK, P], U32, name=f"pair_picked{d}_{b}", align_bytes=64, offset=offset)
-            window = pair_wins[d][:].rearrange("p t e -> p (t e)").bitcast(U32)
+        def gather_couple(d, b, bank):
+            picked = place([P, PACK, P], U32, f"couple_picked{d}_{b}", PICKED_AT + (2 * (d - 2) + b) * 2048)
+            window = couple_wins[d][:].rearrange("p t e -> p (t e)").bitcast(U32)
             nc.vector.tensor_copy(picked[:].rearrange("n t q -> n q t"), window.indirect(picks(b)))
-            turned = turn_psum.tile([P, 2, J_PASSES, P], F32, name="turned")
-            bank = turned[:].rearrange("q u v n -> q (u v) n")
+            turned = bank_tile([P, PACK, P], f"couple_turned{d}_{b}", bank)
             for t in range(PACK):
-                nc.tensor.transpose(bank[:, t, :], picked[:, t, :].bitcast(F32), ident[:])
-            banks[d, b] = bank
+                nc.tensor.transpose(turned[:, t, :], picked[:, t, :].bitcast(F32), ident[:])
+            banks[d, b] = turned[:]
 
-        def part_pair(d, b, halves):
-            signs = sign16[:, b].rearrange("p u e -> p (u e)")
+        def part_couple(d, b, halves):
             count = halves.stop - halves.start
             nc.vector.tensor_tensor(
-                wd16s[d][:, halves, b],
-                signs.unsqueeze(1).unsqueeze(1).to_broadcast([P, count, P, PACK]),
+                wd16s[2 * d][0][:, halves, b],
+                sign16[:, b].unsqueeze(1).unsqueeze(1).to_broadcast([P, count, P, PACK]),
                 banks[d, b].bitcast(BF16).rearrange("q t (n e) -> q e n t", e=2)[:, halves],
                 ALU.mult,
             )
 
-        def quantize_wd(d, halves, offset=None):
-            if d not in wd_codes:
-                wd_codes[d] = keep.tile([P, 2, J_PASSES, P], U32, name=f"wd_code{d}", align_bytes=64)
-                if offset is None:
-                    wd_scales[d] = keep.tile([P, 2, J_PASSES, P], U8, name=f"wd_scale{d}", align_bytes=64)
-                else:
-                    wd_scales[d] = shared.tile(
-                        [P, 2, J_PASSES, P], U8, name=f"wd_scale{d}", align_bytes=64, offset=offset
-                    )
+        def quantize_wd(first_tile, count, offset=None):
+            tile, e = wd16s[first_tile]
+            codes = place([P, count, J_PASSES, P], U32, f"wd_code{first_tile}")
+            scales = place([P, count, J_PASSES, P], U8, f"wd_scale{first_tile}", offset)
             nc.vector.quantize_mx(
-                out=wd_codes[d][:, halves].rearrange("p e b n -> p (e b n)").bitcast(FP8X4),
-                scales=wd_scales[d][:, halves].rearrange("p e b n -> p (e b n)"),
-                in_=wd16s[d][:, halves].rearrange("p e b n t -> p (e b n t)"),
+                out=codes[:].rearrange("p e b n -> p (e b n)").bitcast(FP8X4),
+                scales=scales[:].rearrange("p e b n -> p (e b n)"),
+                in_=tile[:, e : e + count].rearrange("p e b n t -> p (e b n t)"),
             )
+            for k in range(count):
+                wd_codes[first_tile + k], wd_scales[first_tile + k] = codes[:, k], scales[:, k]
 
-        def down(i, mh, on_vector=False):
-            y = sum_psum.tile([P, M_TILE], F32, name="acc")
+        def down(i, mh, bank, offset=None, on_vector=False):
+            y = bank_tile([P, M_TILE], f"down{i}_{mh}", bank)
             for b in range(J_PASSES):
                 nc.tensor.matmul_mx(
                     out=y[:],
-                    lhsT=wd_codes[i // 2][:, i % 2, b, :].bitcast(FP8X4),
-                    lhsT_scale=wd_scales[i // 2][:, i % 2, b, :],
+                    lhsT=wd_codes[i][:, b, :].bitcast(FP8X4),
+                    lhsT_scale=wd_scales[i][:, b, :],
                     rhs=h_codes[mh][:, b].bitcast(FP8X4),
                     rhs_scale=h_scales[mh, b],
                     start=(b == 0),
                     stop=(b == J_PASSES - 1),
                 )
-            if mh == 0 and i < DIRECT:
-                result = shared.tile(
-                    [P, M_TILE], F32, name=f"result{i}", align_bytes=64, offset=Z_AT + WIN_BYTES + i * 4 * M_TILE
-                )
-            else:
+            if offset is None:
                 result = stage.tile([P, M_TILE], F32, name="result")
+            else:
+                result = place([P, M_TILE], F32, f"result{i}", offset)
             if on_vector:
                 nc.vector.tensor_scalar(result[:], y[:], bias[:, i : i + 1], None, ALU.add)
             else:
@@ -287,48 +281,52 @@ def tile_list_sparse_relu2_ffn_kernel(tc, tab_words, tab_scales, offs, x_words, 
             nc.sync.dma_start(out=out_rows[i][:, mh * M_TILE : (mh + 1) * M_TILE], in_=result[:])
 
         both, first, second = slice(0, 2), slice(0, 1), slice(1, 2)
-        for mh in range(M_TILES):
-            for b in range(J_PASSES):
-                make_h(mh, b)
-        for d in PAIRED:
-            cast_pair(d)
-        duo_tile(0, WIN_BYTES)
-        duo_tile(1)
-        duo_tile(2)
-        duo_tile(3)
-        gather_wd(0)
-        gather_wd(1)
-        turn_wd(0)
-        turn_wd(1)
-        quantize_wd(0, both)
-        gather_wd(2)
+        for d in COUPLES:
+            cast_couple(d)
+        rounded_tile(0, 2, WIN_BYTES)
+        rounded_tile(2, 1)
+        rounded_tile(3, 1, PICKED_AT + 2 * 2048)
+        rounded_tile(4, 2)
+        rounded_tile(6, 2)
+        make_h(0, 0)
+        make_h(0, 1)
+        make_h(1, 0)
+        gather_single(0)
+        gather_single(1)
+        turn_single(0, 6)
+        turn_single(1, 7)
+        quantize_wd(0, 2)
+        gather_single(2)
         quantize_h(0, both, 2 * WIN_BYTES)
-        turn_wd(2)
-        gather_wd(3)
-        quantize_h(1, first, 3 * WIN_BYTES + 4096)
-        turn_wd(3)
-        gather_pair(2, 0, 3 * WIN_BYTES)
-        quantize_wd(1, both)
-        gather_pair(2, 1, 3 * WIN_BYTES + 2048)
-        for i in range(DIRECT):
-            down(i, 0)
-        quantize_h(1, second, DIRECT * WIN_BYTES)
-        for i in range(DIRECT):
-            down(i, 1)
-        part_pair(2, 0, both)
-        part_pair(2, 1, both)
-        gather_pair(3, 0)
-        gather_pair(3, 1)
-        quantize_wd(2, both, (DIRECT + 1) * WIN_BYTES)
-        for i in range(DIRECT, DIRECT + 2):
-            down(i, 0)
-            down(i, 1)
-        part_pair(3, 0, both)
-        part_pair(3, 1, first)
-        quantize_wd(3, first)
-        part_pair(3, 1, second)
-        quantize_wd(3, second)
-        down(6, 0)
-        down(6, 1)
-        down(7, 0, on_vector=True)
-        down(7, 1)
+        turn_single(2, 2)
+        make_h(1, 1)
+        quantize_wd(2, 1)
+        gather_couple(2, 0, 6)
+        gather_couple(2, 1, 7)
+        quantize_h(1, first, PICKED_AT)
+        part_couple(2, 0, both)
+        part_couple(2, 1, both)
+        quantize_h(1, second, PICKED_AT + 2048)
+        quantize_wd(4, 2, LAST_H_AT)
+        for k, (i, bank) in enumerate(((2, 0), (0, 6), (1, 7))):
+            down(i, 0, bank, Z_AT + WIN_BYTES + k * 4 * M_TILE)
+        for i, mh, bank in ((0, 1, 4), (1, 1, 5), (2, 1, 1), (4, 0, 2), (4, 1, 3), (5, 0, 0)):
+            down(i, mh, bank)
+        gather_single(3, LAST_H_AT + 2048)
+        gather_couple(3, 0, 6)
+        gather_couple(3, 1, 7)
+        turn_single(3, 4)
+        down(5, 1, 4)
+        part_couple(3, 0, first)
+        quantize_wd(3, 1)
+        down(3, 0, 5)
+        down(3, 1, 1)
+        part_couple(3, 1, first)
+        part_couple(3, 0, second)
+        quantize_wd(6, 1)
+        part_couple(3, 1, second)
+        quantize_wd(7, 1)
+        down(6, 0, 2)
+        down(6, 1, 3)
+        down(7, 0, 0, on_vector=True)
+        down(7, 1, 4)

@@ -37,9 +37,7 @@ BANK_BYTES = 2048
 RING = 6
 Z_AT = COUPLE_AT + len(COUPLES) * WIN_BYTES
 H_AT = Z_AT + J_PASSES * WIN_BYTES
-LAST_H_AT = H_AT + WIN_BYTES + WIN_BYTES // 2
 RAW_AT = H_AT + M_TILES * WIN_BYTES
-PICKED_AT = RAW_AT + 4 * WIN_BYTES
 
 
 def tile_list_sparse_relu2_ffn_kernel(tc, tab_words, tab_scales, offs, x_words, x_scales, g, wdT, bd, out):
@@ -64,7 +62,7 @@ def tile_list_sparse_relu2_ffn_kernel(tc, tab_words, tab_scales, offs, x_words, 
         gain = keep.tile([P, J_PASSES, PACK], F32, name="gain")
         nc.sync.dma_start(out=gain[:], in_=g.rearrange("(b p t) -> p b t", p=P, t=PACK))
         tab_plane = place([P, T], U8, "tab_plane")
-        x_plane = place([P, K_PASSES, M], U8, "x_plane")
+        x_plane = place([P, M], U8, "x_plane")
         nc.gpsimd.memset(tab_plane[:].bitcast(I32), 0)
         nc.gpsimd.memset(x_plane[:].bitcast(I32), 0)
         for q in range(QUADS):
@@ -84,8 +82,8 @@ def tile_list_sparse_relu2_ffn_kernel(tc, tab_words, tab_scales, offs, x_words, 
         load_table(0)
         for q in range(QUADS):
             nc.sync.dma_start(
-                out=x_plane[32 * q : 32 * q + 4].bitcast(I32),
-                in_=x_scales[:, 4 * q : 4 * q + 4, :].rearrange("a r c -> r a c").bitcast(I32),
+                out=x_plane[32 * q : 32 * q + 4 * K_PASSES, :].bitcast(I32),
+                in_=x_scales[:, 4 * q : 4 * q + 4, :].bitcast(I32),
             )
         load_table(1)
 
@@ -108,9 +106,9 @@ def tile_list_sparse_relu2_ffn_kernel(tc, tab_words, tab_scales, offs, x_words, 
         bias = keep.tile([P, N_TILES], F32, name="bias")
         nc.sync.dma_start(out=bias[:], in_=bd.rearrange("(p i) -> p i", i=N_TILES))
         load_single(2)
+        load_single(3)
         load_couple_part(2, 1)
         load_couple_part(3, 0)
-        load_single(3)
         load_couple_part(3, 1)
 
         ident = keep.tile([P, P], F32, name="ident")
@@ -153,7 +151,7 @@ def tile_list_sparse_relu2_ffn_kernel(tc, tab_words, tab_scales, offs, x_words, 
                 lhsT=v_codes[b, a][:, t, :].bitcast(FP8X4),
                 lhsT_scale=v_scale[4 * a :, b, t, :],
                 rhs=x_codes.bitcast(FP8X4),
-                rhs_scale=x_plane[:, a, mh * M_TILE : (mh + 1) * M_TILE],
+                rhs_scale=x_plane[4 * a :, mh * M_TILE : (mh + 1) * M_TILE],
                 start=(a == 0),
                 stop=(a == K_PASSES - 1),
             )
@@ -228,14 +226,18 @@ def tile_list_sparse_relu2_ffn_kernel(tc, tab_words, tab_scales, offs, x_words, 
                     raw[d, c][:, :, lo : lo + CAST_COLS].rearrange("p e (c i) -> p c e i", i=4),
                 )
 
-        def gather_couple(d, b, bank):
-            picked = place([P, PACK, P], U32, f"couple_picked{d}_{b}", PICKED_AT + (2 * (d - 2) + b) * 2048)
+        def gather_couple(d, passes, first_bank):
+            count = passes.stop - passes.start
+            picked = place([P, count, PACK, P], U32, f"couple_picked{d}_{passes.start}")
             window = couple_wins[d][:].rearrange("p t e -> p (t e)").bitcast(U32)
-            nc.vector.tensor_copy(picked[:].rearrange("n t q -> n q t"), window.indirect(picks(b)))
-            turned = bank_tile([P, PACK, P], f"couple_turned{d}_{b}", bank)
-            for t in range(PACK):
-                nc.tensor.transpose(turned[:, t, :], picked[:, t, :].bitcast(F32), ident[:])
-            banks[d, b] = turned[:]
+            listed = offsets[:, passes.start * LIST_COLS : passes.stop * LIST_COLS]
+            nc.vector.tensor_copy(picked[:].rearrange("n b t q -> n b q t"), window.indirect(listed))
+            for k in range(count):
+                b = passes.start + k
+                turned = bank_tile([P, PACK, P], f"couple_turned{d}_{b}", first_bank + k)
+                for t in range(PACK):
+                    nc.tensor.transpose(turned[:, t, :], picked[:, k, t, :].bitcast(F32), ident[:])
+                banks[d, b] = turned[:]
 
         def part_couple(d, b, halves):
             count = halves.stop - halves.start
@@ -284,49 +286,44 @@ def tile_list_sparse_relu2_ffn_kernel(tc, tab_words, tab_scales, offs, x_words, 
         for d in COUPLES:
             cast_couple(d)
         rounded_tile(0, 2, WIN_BYTES)
-        rounded_tile(2, 1)
-        rounded_tile(3, 1, PICKED_AT + 2 * 2048)
+        rounded_tile(2, 2, 3 * WIN_BYTES)
         rounded_tile(4, 2)
         rounded_tile(6, 2)
-        make_h(0, 0)
-        make_h(0, 1)
-        make_h(1, 0)
+        for mh in range(M_TILES):
+            for b in range(J_PASSES):
+                make_h(mh, b)
         gather_single(0)
         gather_single(1)
         turn_single(0, 6)
         turn_single(1, 7)
         quantize_wd(0, 2)
         gather_single(2)
-        quantize_h(0, both, 2 * WIN_BYTES)
-        turn_single(2, 2)
-        make_h(1, 1)
-        quantize_wd(2, 1)
-        gather_couple(2, 0, 6)
-        gather_couple(2, 1, 7)
-        quantize_h(1, first, PICKED_AT)
+        gather_single(3)
+        quantize_h(0, both, 3 * WIN_BYTES + 4096)
+        turn_single(2, 6)
+        turn_single(3, 7)
+        quantize_wd(2, 2)
+        for i, bank in enumerate((4, 5, 0, 1)):
+            down(i, 0, bank, Z_AT + WIN_BYTES + i * 4 * M_TILE)
+        gather_couple(2, both, 6)
+        quantize_h(1, both, COUPLE_AT)
         part_couple(2, 0, both)
         part_couple(2, 1, both)
-        quantize_h(1, second, PICKED_AT + 2048)
-        quantize_wd(4, 2, LAST_H_AT)
-        for k, (i, bank) in enumerate(((2, 0), (0, 6), (1, 7))):
-            down(i, 0, bank, Z_AT + WIN_BYTES + k * 4 * M_TILE)
-        for i, mh, bank in ((0, 1, 4), (1, 1, 5), (2, 1, 1), (4, 0, 2), (4, 1, 3), (5, 0, 0)):
-            down(i, mh, bank)
-        gather_single(3, LAST_H_AT + 2048)
-        gather_couple(3, 0, 6)
-        gather_couple(3, 1, 7)
-        turn_single(3, 4)
-        down(5, 1, 4)
-        part_couple(3, 0, first)
-        quantize_wd(3, 1)
-        down(3, 0, 5)
-        down(3, 1, 1)
+        quantize_wd(4, 2)
+        for i, bank in enumerate((2, 3, 6, 7)):
+            down(i, 1, bank)
+        down(4, 0, 4)
+        down(4, 1, 5)
+        down(5, 0, 0)
+        gather_couple(3, first, 1)
+        gather_couple(3, second, 2)
+        part_couple(3, 0, both)
+        down(5, 1, 1)
         part_couple(3, 1, first)
-        part_couple(3, 0, second)
         quantize_wd(6, 1)
         part_couple(3, 1, second)
         quantize_wd(7, 1)
-        down(6, 0, 2)
-        down(6, 1, 3)
-        down(7, 0, 0, on_vector=True)
+        down(6, 0, 3)
+        down(6, 1, 6)
+        down(7, 0, 7, on_vector=True)
         down(7, 1, 4)

@@ -31,13 +31,13 @@ SQRT_FLOOR = 2.0**-116
 SINGLES = 4
 COUPLES = (2, 3)
 LOAD_COLS = 1024
-CAST_COLS = 512
 COUPLE_AT = SINGLES * WIN_BYTES
 BANK_BYTES = 2048
 RING = 6
 Z_AT = COUPLE_AT + len(COUPLES) * WIN_BYTES
 H_AT = Z_AT + J_PASSES * WIN_BYTES
 RAW_AT = H_AT + M_TILES * WIN_BYTES
+LAST_H_AT = H_AT + WIN_BYTES + WIN_BYTES // 2
 
 
 def tile_list_sparse_relu2_ffn_kernel(tc, tab_words, tab_scales, offs, x_words, x_scales, g, wdT, bd, out):
@@ -72,12 +72,15 @@ def tile_list_sparse_relu2_ffn_kernel(tc, tab_words, tab_scales, offs, x_words, 
             )
         tab = [place([P, T], I32, f"tab{a}") for a in range(K_PASSES)]
         x_view = x_words.rearrange("a p c i -> p a (c i)").bitcast(I32)
-        x_first = [place([P, M_TILE], I32, f"x_first{a}") for a in range(K_PASSES)]
-        x_second = place([P, K_PASSES, M_TILE], I32, "x_second")
+        x_codes = {}
+
+        def load_x(mh, a):
+            x_codes[mh, a] = place([P, M_TILE], I32, f"x{mh}_{a}")
+            nc.sync.dma_start(out=x_codes[mh, a][:], in_=x_view[:, a, mh * M_TILE : (mh + 1) * M_TILE])
 
         def load_table(a):
             nc.sync.dma_start(out=tab[a][:], in_=tab_words[a].rearrange("p t i -> p (t i)").bitcast(I32))
-            nc.sync.dma_start(out=x_first[a][:], in_=x_view[:, a, 0:M_TILE])
+            load_x(0, a)
 
         load_table(0)
         for q in range(QUADS):
@@ -102,12 +105,13 @@ def tile_list_sparse_relu2_ffn_kernel(tc, tab_words, tab_scales, offs, x_words, 
         load_single(0)
         load_single(1)
         load_couple_part(2, 0)
-        nc.sync.dma_start(out=x_second[:], in_=x_view[:, :, M_TILE:M])
+        load_x(1, 0)
+        load_single(2)
+        load_x(1, 1)
         bias = keep.tile([P, N_TILES], F32, name="bias")
         nc.sync.dma_start(out=bias[:], in_=bd.rearrange("(p i) -> p i", i=N_TILES))
-        load_single(2)
-        load_single(3)
         load_couple_part(2, 1)
+        load_single(3)
         load_couple_part(3, 0)
         load_couple_part(3, 1)
 
@@ -145,12 +149,11 @@ def tile_list_sparse_relu2_ffn_kernel(tc, tab_words, tab_scales, offs, x_words, 
         pickeds, wd16s, wd_codes, wd_scales = {}, {}, {}, {}
 
         def up_pass(acc, mh, b, t, a):
-            x_codes = x_first[a][:] if mh == 0 else x_second[:, a, :]
             nc.tensor.matmul_mx(
                 out=acc[:],
                 lhsT=v_codes[b, a][:, t, :].bitcast(FP8X4),
                 lhsT_scale=v_scale[4 * a :, b, t, :],
-                rhs=x_codes.bitcast(FP8X4),
+                rhs=x_codes[mh, a][:].bitcast(FP8X4),
                 rhs_scale=x_plane[4 * a :, mh * M_TILE : (mh + 1) * M_TILE],
                 start=(a == 0),
                 stop=(a == K_PASSES - 1),
@@ -160,12 +163,12 @@ def tile_list_sparse_relu2_ffn_kernel(tc, tab_words, tab_scales, offs, x_words, 
             z = place([P, PACK, M_TILE], F32, f"z{mh}_{b}", Z_AT + b * WIN_BYTES)
             group = (mh * J_PASSES + b) * PACK
             accs = [bank_tile([P, M_TILE], f"up{group + t}", (group + t) % RING) for t in range(PACK)]
-            if group == 0:
+            if b == 0:
                 for t in range(PACK):
                     up_pass(accs[t], mh, b, t, 0)
             for t in range(PACK):
                 acc = accs[t]
-                if group > 0:
+                if b > 0:
                     up_pass(acc, mh, b, t, 0)
                 up_pass(acc, mh, b, t, 1)
                 col = b * PACK + t
@@ -206,6 +209,10 @@ def tile_list_sparse_relu2_ffn_kernel(tc, tab_words, tab_scales, offs, x_words, 
             for b in range(J_PASSES):
                 for u in range(2):
                     nc.tensor.transpose(turned[:, u, b, :], words[:, u, b * P : (b + 1) * P], ident[:])
+            banks[i] = turned
+
+        def sign_single(i):
+            turned = banks[i]
             tile, e = wd16s[i]
             signs = sign16[:].rearrange("p b (u e) -> p b u e", e=2)
             nc.vector.tensor_tensor(
@@ -219,16 +226,15 @@ def tile_list_sparse_relu2_ffn_kernel(tc, tab_words, tab_scales, offs, x_words, 
 
         def cast_couple(d):
             couple_wins[d] = place([P, T, 2], BF16, f"couple_win{d}", COUPLE_AT + (d - 2) * WIN_BYTES)
-            for c0 in range(0, T, CAST_COLS):
-                c, lo = divmod(c0, LOAD_COLS)
+            for c in range(T // LOAD_COLS):
                 nc.gpsimd.tensor_copy(
-                    couple_wins[d][:, c0 : c0 + CAST_COLS, :].rearrange("p (c i) e -> p c e i", i=4),
-                    raw[d, c][:, :, lo : lo + CAST_COLS].rearrange("p e (c i) -> p c e i", i=4),
+                    couple_wins[d][:, c * LOAD_COLS : (c + 1) * LOAD_COLS, :].rearrange("p (c i) e -> p c e i", i=4),
+                    raw[d, c][:].rearrange("p e (c i) -> p c e i", i=4),
                 )
 
-        def gather_couple(d, passes, first_bank):
+        def gather_couple(d, passes, first_bank, offset=None):
             count = passes.stop - passes.start
-            picked = place([P, count, PACK, P], U32, f"couple_picked{d}_{passes.start}")
+            picked = place([P, count, PACK, P], U32, f"couple_picked{d}_{passes.start}", offset)
             window = couple_wins[d][:].rearrange("p t e -> p (t e)").bitcast(U32)
             listed = offsets[:, passes.start * LIST_COLS : passes.stop * LIST_COLS]
             nc.vector.tensor_copy(picked[:].rearrange("n b t q -> n b q t"), window.indirect(listed))
@@ -286,44 +292,52 @@ def tile_list_sparse_relu2_ffn_kernel(tc, tab_words, tab_scales, offs, x_words, 
         for d in COUPLES:
             cast_couple(d)
         rounded_tile(0, 2, WIN_BYTES)
-        rounded_tile(2, 2, 3 * WIN_BYTES)
+        rounded_tile(2, 1)
+        rounded_tile(3, 1, 3 * WIN_BYTES)
         rounded_tile(4, 2)
         rounded_tile(6, 2)
-        for mh in range(M_TILES):
-            for b in range(J_PASSES):
-                make_h(mh, b)
+        make_h(0, 0)
+        make_h(0, 1)
+        make_h(1, 0)
         gather_single(0)
         gather_single(1)
         turn_single(0, 6)
         turn_single(1, 7)
+        sign_single(0)
+        sign_single(1)
         quantize_wd(0, 2)
         gather_single(2)
+        quantize_h(0, both, 2 * WIN_BYTES)
+        turn_single(2, 2)
+        sign_single(2)
+        make_h(1, 1)
+        quantize_wd(2, 1)
         gather_single(3)
-        quantize_h(0, both, 3 * WIN_BYTES + 4096)
-        turn_single(2, 6)
-        turn_single(3, 7)
-        quantize_wd(2, 2)
-        for i, bank in enumerate((4, 5, 0, 1)):
-            down(i, 0, bank, Z_AT + WIN_BYTES + i * 4 * M_TILE)
-        gather_couple(2, both, 6)
-        quantize_h(1, both, COUPLE_AT)
+        turn_single(3, 4)
+        gather_couple(2, first, 6, 3 * WIN_BYTES)
+        gather_couple(2, second, 7, 3 * WIN_BYTES + 2048)
+        sign_single(3)
         part_couple(2, 0, both)
+        quantize_wd(3, 1)
+        quantize_h(1, both, 3 * WIN_BYTES + 2048)
         part_couple(2, 1, both)
-        quantize_wd(4, 2)
-        for i, bank in enumerate((2, 3, 6, 7)):
+        quantize_wd(4, 2, LAST_H_AT)
+        for k, (i, bank) in enumerate(((0, 5), (1, 0), (2, 4), (3, 6))):
+            down(i, 0, bank, Z_AT + WIN_BYTES + k * 4 * M_TILE)
+        for i, bank in enumerate((1, 2, 3, 7)):
             down(i, 1, bank)
-        down(4, 0, 4)
-        down(4, 1, 5)
-        down(5, 0, 0)
-        gather_couple(3, first, 1)
-        gather_couple(3, second, 2)
+        down(4, 0, 5)
+        down(4, 1, 0)
+        gather_couple(3, first, 4, H_AT + WIN_BYTES)
+        gather_couple(3, second, 6, H_AT + WIN_BYTES + 2048)
+        down(5, 0, 1)
         part_couple(3, 0, both)
-        down(5, 1, 1)
+        down(5, 1, 4)
         part_couple(3, 1, first)
         quantize_wd(6, 1)
         part_couple(3, 1, second)
         quantize_wd(7, 1)
-        down(6, 0, 3)
-        down(6, 1, 6)
+        down(6, 0, 2)
+        down(6, 1, 3)
         down(7, 0, 7, on_vector=True)
-        down(7, 1, 4)
+        down(7, 1, 5)

@@ -32,6 +32,7 @@ SINGLES = 4
 COUPLES = (2, 3)
 LOAD_COLS = 1024
 COUPLE_AT = SINGLES * WIN_BYTES
+SCALAR_COLS = 128
 BANK_BYTES = 2048
 RING = 6
 Z_AT = COUPLE_AT + len(COUPLES) * WIN_BYTES
@@ -104,10 +105,10 @@ def tile_list_sparse_relu2_ffn_kernel(tc, tab_words, tab_scales, offs, x_words, 
 
         load_single(0)
         load_single(1)
-        load_couple_part(2, 0)
         load_x(1, 0)
-        load_single(2)
         load_x(1, 1)
+        load_single(2)
+        load_couple_part(2, 0)
         bias = keep.tile([P, N_TILES], F32, name="bias")
         nc.sync.dma_start(out=bias[:], in_=bd.rearrange("(p i) -> p i", i=N_TILES))
         load_couple_part(2, 1)
@@ -160,7 +161,7 @@ def tile_list_sparse_relu2_ffn_kernel(tc, tab_words, tab_scales, offs, x_words, 
             )
 
         def make_h(mh, b):
-            z = place([P, PACK, M_TILE], F32, f"z{mh}_{b}", Z_AT + b * WIN_BYTES)
+            z = place([P, PACK, M_TILE], F32, f"z{mh}_{b}", Z_AT + b * WIN_BYTES if mh + b else None)
             group = (mh * J_PASSES + b) * PACK
             accs = [bank_tile([P, M_TILE], f"up{group + t}", (group + t) % RING) for t in range(PACK)]
             if b == 0:
@@ -175,11 +176,17 @@ def tile_list_sparse_relu2_ffn_kernel(tc, tab_words, tab_scales, offs, x_words, 
                 nc.scalar.activation(z[:, t, :], acc[:], ACT.Relu, scale=root[:, col : col + 1])
             if mh not in h16s:
                 h16s[mh] = place([P, J_PASSES, M_TILE, PACK], BF16, f"h16_{mh}", H_AT + mh * WIN_BYTES)
+            split = SCALAR_COLS if group == 0 else M_TILE
             nc.scalar.activation(
-                h16s[mh][:, b].rearrange("p (c i) t -> p c t i", i=4),
-                z[:].rearrange("p t (c i) -> p c t i", i=4),
+                h16s[mh][:, b, :split].rearrange("p (c i) t -> p c t i", i=4),
+                z[:, :, :split].rearrange("p t (c i) -> p c t i", i=4),
                 ACT.Square,
             )
+            if split < M_TILE:
+                rest = z[:, :, split:].rearrange("p t (c i) -> p c t i", i=4)
+                nc.gpsimd.tensor_tensor(
+                    h16s[mh][:, b, split:].rearrange("p (c i) t -> p c t i", i=4), rest, rest, ALU.mult
+                )
 
         def quantize_h(mh, passes, offset=None):
             if mh not in h_codes:
@@ -289,14 +296,14 @@ def tile_list_sparse_relu2_ffn_kernel(tc, tab_words, tab_scales, offs, x_words, 
             nc.sync.dma_start(out=out_rows[i][:, mh * M_TILE : (mh + 1) * M_TILE], in_=result[:])
 
         both, first, second = slice(0, 2), slice(0, 1), slice(1, 2)
-        for d in COUPLES:
-            cast_couple(d)
         rounded_tile(0, 2, WIN_BYTES)
         rounded_tile(2, 1)
         rounded_tile(3, 1, 3 * WIN_BYTES)
         rounded_tile(4, 2)
         rounded_tile(6, 2)
         make_h(0, 0)
+        for d in COUPLES:
+            cast_couple(d)
         make_h(0, 1)
         make_h(1, 0)
         gather_single(0)

@@ -31,6 +31,7 @@ SQRT_FLOOR = 2.0**-116
 SINGLES = 4
 COUPLES = (2, 3)
 LOAD_COLS = 1024
+CAST_COLS = 512
 COUPLE_AT = SINGLES * WIN_BYTES
 SCALAR_COLS = 128
 BANK_BYTES = 2048
@@ -75,21 +76,18 @@ def tile_list_sparse_relu2_ffn_kernel(tc, tab_words, tab_scales, offs, x_words, 
         x_view = x_words.rearrange("a p c i -> p a (c i)").bitcast(I32)
         x_codes = {}
 
-        def load_x(mh, a):
-            x_codes[mh, a] = place([P, M_TILE], I32, f"x{mh}_{a}")
-            nc.sync.dma_start(out=x_codes[mh, a][:], in_=x_view[:, a, mh * M_TILE : (mh + 1) * M_TILE])
+        def load_x(mh):
+            x_codes[mh] = place([P, K_PASSES, M_TILE], I32, f"x{mh}")
+            nc.sync.dma_start(out=x_codes[mh][:], in_=x_view[:, :, mh * M_TILE : (mh + 1) * M_TILE])
 
-        def load_table(a):
+        for a in range(K_PASSES):
             nc.sync.dma_start(out=tab[a][:], in_=tab_words[a].rearrange("p t i -> p (t i)").bitcast(I32))
-            load_x(0, a)
-
-        load_table(0)
+        load_x(0)
         for q in range(QUADS):
             nc.sync.dma_start(
                 out=x_plane[32 * q : 32 * q + 4 * K_PASSES, :].bitcast(I32),
                 in_=x_scales[:, 4 * q : 4 * q + 4, :].bitcast(I32),
             )
-        load_table(1)
 
         wd_rows = wdT.rearrange("(p i) t -> p i t", i=N_TILES)
         out_rows = out.rearrange("(p i) m -> i p m", i=N_TILES)
@@ -105,8 +103,7 @@ def tile_list_sparse_relu2_ffn_kernel(tc, tab_words, tab_scales, offs, x_words, 
 
         load_single(0)
         load_single(1)
-        load_x(1, 0)
-        load_x(1, 1)
+        load_x(1)
         load_single(2)
         load_couple_part(2, 0)
         bias = keep.tile([P, N_TILES], F32, name="bias")
@@ -139,8 +136,8 @@ def tile_list_sparse_relu2_ffn_kernel(tc, tab_words, tab_scales, offs, x_words, 
         v_scale = place([P, J_PASSES, PACK, P], U8, "v_scale")
         nc.vector.tensor_copy(v_scale[:].rearrange("k b t p -> k b p t"), tab_plane[:].indirect(offsets[:]))
         v_codes = {}
-        for a in range(K_PASSES):
-            for b in range(J_PASSES):
+        for b in range(J_PASSES):
+            for a in range(K_PASSES):
                 v_codes[b, a] = place([P, PACK, P], U32, f"v_code{b}_{a}")
                 nc.vector.tensor_copy(
                     v_codes[b, a][:].rearrange("k t p -> k p t"), tab[a][:].bitcast(U32).indirect(picks(b))
@@ -154,7 +151,7 @@ def tile_list_sparse_relu2_ffn_kernel(tc, tab_words, tab_scales, offs, x_words, 
                 out=acc[:],
                 lhsT=v_codes[b, a][:, t, :].bitcast(FP8X4),
                 lhsT_scale=v_scale[4 * a :, b, t, :],
-                rhs=x_codes[mh, a][:].bitcast(FP8X4),
+                rhs=x_codes[mh][:, a, :].bitcast(FP8X4),
                 rhs_scale=x_plane[4 * a :, mh * M_TILE : (mh + 1) * M_TILE],
                 start=(a == 0),
                 stop=(a == K_PASSES - 1),
@@ -164,14 +161,10 @@ def tile_list_sparse_relu2_ffn_kernel(tc, tab_words, tab_scales, offs, x_words, 
             z = place([P, PACK, M_TILE], F32, f"z{mh}_{b}", Z_AT + b * WIN_BYTES if mh + b else None)
             group = (mh * J_PASSES + b) * PACK
             accs = [bank_tile([P, M_TILE], f"up{group + t}", (group + t) % RING) for t in range(PACK)]
-            if b == 0:
-                for t in range(PACK):
-                    up_pass(accs[t], mh, b, t, 0)
             for t in range(PACK):
                 acc = accs[t]
-                if b > 0:
-                    up_pass(acc, mh, b, t, 0)
-                up_pass(acc, mh, b, t, 1)
+                for a in range(K_PASSES):
+                    up_pass(acc, mh, b, t, a)
                 col = b * PACK + t
                 nc.scalar.activation(z[:, t, :], acc[:], ACT.Relu, scale=root[:, col : col + 1])
             if mh not in h16s:
@@ -233,10 +226,11 @@ def tile_list_sparse_relu2_ffn_kernel(tc, tab_words, tab_scales, offs, x_words, 
 
         def cast_couple(d):
             couple_wins[d] = place([P, T, 2], BF16, f"couple_win{d}", COUPLE_AT + (d - 2) * WIN_BYTES)
-            for c in range(T // LOAD_COLS):
+            for c0 in range(0, T, CAST_COLS):
+                c, lo = divmod(c0, LOAD_COLS)
                 nc.gpsimd.tensor_copy(
-                    couple_wins[d][:, c * LOAD_COLS : (c + 1) * LOAD_COLS, :].rearrange("p (c i) e -> p c e i", i=4),
-                    raw[d, c][:].rearrange("p e (c i) -> p c e i", i=4),
+                    couple_wins[d][:, c0 : c0 + CAST_COLS, :].rearrange("p (c i) e -> p c e i", i=4),
+                    raw[d, c][:, :, lo : lo + CAST_COLS].rearrange("p e (c i) -> p c e i", i=4),
                 )
 
         def gather_couple(d, passes, first_bank, offset=None):
@@ -312,11 +306,11 @@ def tile_list_sparse_relu2_ffn_kernel(tc, tab_words, tab_scales, offs, x_words, 
         turn_single(1, 7)
         sign_single(0)
         sign_single(1)
-        quantize_wd(0, 2)
-        gather_single(2)
-        quantize_h(0, both, 2 * WIN_BYTES)
+        gather_single(2, 0)
+        quantize_wd(0, 2, 2 * WIN_BYTES)
         turn_single(2, 2)
         sign_single(2)
+        quantize_h(0, both, 0)
         make_h(1, 1)
         quantize_wd(2, 1)
         gather_single(3)

@@ -103,9 +103,9 @@ def tile_list_sparse_relu2_ffn_kernel(tc, tab_words, tab_scales, offs, x_words, 
 
         load_single(0)
         load_single(1)
+        load_couple_part(2, 0)
         load_x(1)
         load_single(2)
-        load_couple_part(2, 0)
         bias = keep.tile([P, N_TILES], F32, name="bias")
         nc.sync.dma_start(out=bias[:], in_=bd.rearrange("(p i) -> p i", i=N_TILES))
         load_couple_part(2, 1)
@@ -291,8 +291,7 @@ def tile_list_sparse_relu2_ffn_kernel(tc, tab_words, tab_scales, offs, x_words, 
 
         both, first, second = slice(0, 2), slice(0, 1), slice(1, 2)
         rounded_tile(0, 2, WIN_BYTES)
-        rounded_tile(2, 1)
-        rounded_tile(3, 1, 3 * WIN_BYTES)
+        rounded_tile(2, 2)
         rounded_tile(4, 2)
         rounded_tile(6, 2)
         make_h(0, 0)
@@ -306,21 +305,21 @@ def tile_list_sparse_relu2_ffn_kernel(tc, tab_words, tab_scales, offs, x_words, 
         turn_single(1, 7)
         sign_single(0)
         sign_single(1)
-        gather_single(2, 0)
-        quantize_wd(0, 2, 2 * WIN_BYTES)
+        quantize_wd(0, 2)
+        gather_single(2)
+        quantize_h(0, both, 2 * WIN_BYTES)
         turn_single(2, 2)
         sign_single(2)
-        quantize_h(0, both, 0)
         make_h(1, 1)
-        quantize_wd(2, 1)
-        gather_single(3)
+        gather_single(3, WIN_BYTES // 2)
+        quantize_h(1, first, 3 * WIN_BYTES)
         turn_single(3, 4)
-        gather_couple(2, first, 6, 3 * WIN_BYTES)
-        gather_couple(2, second, 7, 3 * WIN_BYTES + 2048)
         sign_single(3)
+        gather_couple(2, first, 6, WIN_BYTES // 2 - 1024)
+        gather_couple(2, second, 7, WIN_BYTES // 2 + 1024)
+        quantize_wd(2, 2)
         part_couple(2, 0, both)
-        quantize_wd(3, 1)
-        quantize_h(1, both, 3 * WIN_BYTES + 2048)
+        quantize_h(1, second, WIN_BYTES // 2 + 1024)
         part_couple(2, 1, both)
         quantize_wd(4, 2, LAST_H_AT)
         for k, (i, bank) in enumerate(((0, 5), (1, 0), (2, 4), (3, 6))):

from contextlib import ExitStack

import concourse.mybir as mybir
from concourse.masks import make_identity

K, N, M, T, S = 1024, 1024, 1024, 2048, 1024
FLOPS = 2 * K * S * M + 2 * S * N * M

F32 = mybir.dt.float32
BF16 = mybir.dt.bfloat16
I32 = mybir.dt.int32
U32 = mybir.dt.uint32
U16 = mybir.dt.uint16
U8 = mybir.dt.uint8
FP8X4 = mybir.dt.float8_e4m3fn_x4
ALU = mybir.AluOpType
ACT = mybir.ActivationFunctionType

P = 128
PACK = 4
PASS = P * PACK
K_PASSES = K // PASS
J_PASSES = S // PASS
M_TILE = 512
M_TILES = M // M_TILE
N_TILES = N // P
QUADS = 4
LIST_COLS = PASS // 16
WIN_BYTES = 4 * T
SQRT_FLOOR = 2.0**-116
SINGLES = 4
COUPLES = (2, 3)
LOAD_COLS = 1024
CAST_COLS = 512
COUPLE_AT = SINGLES * WIN_BYTES
SCALAR_COLS = 128
BANK_BYTES = 2048
RING = 6
Z_AT = COUPLE_AT + len(COUPLES) * WIN_BYTES
H_AT = Z_AT + J_PASSES * WIN_BYTES
RAW_AT = H_AT + M_TILES * WIN_BYTES
LAST_H_AT = H_AT + WIN_BYTES + WIN_BYTES // 2


def tile_list_sparse_relu2_ffn_kernel(tc, tab_words, tab_scales, offs, x_words, x_scales, g, wdT, bd, out):
    nc = tc.nc
    with ExitStack() as ctx:
        keep = ctx.enter_context(tc.tile_pool(name="keep", bufs=1))
        shared = ctx.enter_context(tc.tile_pool(name="shared", bufs=1))
        stage = ctx.enter_context(tc.tile_pool(name="stage", bufs=12))
        psum = ctx.enter_context(tc.psum_pool(name="psum", bufs=1))

        def place(shape, dtype, name, offset=None):
            if offset is None:
                return keep.tile(shape, dtype, name=name, align_bytes=64)
            return shared.tile(shape, dtype, name=name, align_bytes=64, offset=offset)

        def bank_tile(shape, name, bank):
            return psum.tile(shape, F32, name=name, offset=bank * BANK_BYTES)

        offsets = keep.tile([P, S // 16], U16, name="offsets")
        nc.sync.dma_start(offsets[:], offs)

        gain = keep.tile([P, J_PASSES, PACK], F32, name="gain")
        nc.sync.dma_start(out=gain[:], in_=g.rearrange("(b p t) -> p b t", p=P, t=PACK))
        tab_plane = place([P, T], U8, "tab_plane")
        x_plane = place([P, M], U8, "x_plane")
        nc.gpsimd.memset(tab_plane[:].bitcast(I32), 0)
        nc.gpsimd.memset(x_plane[:].bitcast(I32), 0)
        for q in range(QUADS):
            nc.sync.dma_start(
                out=tab_plane[32 * q : 32 * q + 4 * K_PASSES, :].bitcast(I32),
                in_=tab_scales[:, 4 * q : 4 * q + 4, :].bitcast(I32),
            )
        tab = [place([P, T], I32, f"tab{a}") for a in range(K_PASSES)]
        x_view = x_words.rearrange("a p c i -> p a (c i)").bitcast(I32)
        x_codes = {}

        def load_x(mh):
            x_codes[mh] = place([P, K_PASSES, M_TILE], I32, f"x{mh}")
            nc.sync.dma_start(out=x_codes[mh][:], in_=x_view[:, :, mh * M_TILE : (mh + 1) * M_TILE])

        for a in range(K_PASSES):
            nc.sync.dma_start(out=tab[a][:], in_=tab_words[a].rearrange("p t i -> p (t i)").bitcast(I32))
        load_x(0)
        for q in range(QUADS):
            nc.sync.dma_start(
                out=x_plane[32 * q : 32 * q + 4 * K_PASSES, :].bitcast(I32),
                in_=x_scales[:, 4 * q : 4 * q + 4, :].bitcast(I32),
            )

        wd_rows = wdT.rearrange("(p i) t -> p i t", i=N_TILES)
        out_rows = out.rearrange("(p i) m -> i p m", i=N_TILES)
        wd_win = [place([P, T], F32, f"wd_win{i}", i * WIN_BYTES) for i in range(SINGLES)]
        raw = {}

        def load_single(i):
            nc.sync.dma_start(out=wd_win[i][:], in_=wd_rows[:, i])

        def load_couple_part(d, c):
            raw[d, c] = place([P, 2, LOAD_COLS], F32, f"raw{d}_{c}", RAW_AT + (2 * (d - 2) + c) * WIN_BYTES)
            nc.sync.dma_start(out=raw[d, c][:], in_=wd_rows[:, 2 * d : 2 * d + 2, c * LOAD_COLS : (c + 1) * LOAD_COLS])

        load_single(0)
        load_single(1)
        load_couple_part(2, 0)
        load_x(1)
        load_single(2)
        bias = keep.tile([P, N_TILES], F32, name="bias")
        nc.sync.dma_start(out=bias[:], in_=bd.rearrange("(p i) -> p i", i=N_TILES))
        load_couple_part(2, 1)
        load_single(3)
        load_couple_part(3, 0)
        load_couple_part(3, 1)

        ident = keep.tile([P, P], F32, name="ident")
        make_identity(nc, ident[:])

        def picks(b):
            return offsets[:, b * LIST_COLS : (b + 1) * LIST_COLS]

        gain_flat = gain[:].rearrange("p b t -> p (b t)")
        width = J_PASSES * PACK
        floor = keep.tile([P, 1], F32, name="floor")
        nc.gpsimd.memset(floor[:], SQRT_FLOOR)
        mag = keep.tile([P, width], F32, name="mag")
        root = keep.tile([P, width], F32, name="root")
        twice_ge = keep.tile([P, width], F32, name="twice_ge")
        sign16 = keep.tile([P, J_PASSES, PACK], BF16, name="sign16")
        sign_flat = sign16[:].rearrange("p b t -> p (b t)")
        nc.gpsimd.tensor_scalar(twice_ge[:], gain_flat, 0.0, 2.0, ALU.is_ge, ALU.mult)
        nc.gpsimd.tensor_scalar(sign_flat, twice_ge[:], 1.0, -1.0, ALU.mult, ALU.add)
        nc.gpsimd.tensor_tensor(mag[:], gain_flat, sign_flat, ALU.mult)
        nc.scalar.activation(root[:], mag[:], ACT.Sqrt, bias=floor[:])

        v_scale = place([P, J_PASSES, PACK, P], U8, "v_scale")
        nc.vector.tensor_copy(v_scale[:].rearrange("k b t p -> k b p t"), tab_plane[:].indirect(offsets[:]))
        v_codes = {}
        for b in range(J_PASSES):
            for a in range(K_PASSES):
                v_codes[b, a] = place([P, PACK, P], U32, f"v_code{b}_{a}")
                nc.vector.tensor_copy(
                    v_codes[b, a][:].rearrange("k t p -> k p t"), tab[a][:].bitcast(U32).indirect(picks(b))
                )

        h16s, h_codes, h_scales = {}, {}, {}
        pickeds, wd16s, wd_codes, wd_scales = {}, {}, {}, {}

        def up_pass(acc, mh, b, t, a):
            nc.tensor.matmul_mx(
                out=acc[:],
                lhsT=v_codes[b, a][:, t, :].bitcast(FP8X4),
                lhsT_scale=v_scale[4 * a :, b, t, :],
                rhs=x_codes[mh][:, a, :].bitcast(FP8X4),
                rhs_scale=x_plane[4 * a :, mh * M_TILE : (mh + 1) * M_TILE],
                start=(a == 0),
                stop=(a == K_PASSES - 1),
            )

        def make_h(mh, b):
            z = place([P, PACK, M_TILE], F32, f"z{mh}_{b}", Z_AT + b * WIN_BYTES if mh + b else None)
            group = (mh * J_PASSES + b) * PACK
            accs = [bank_tile([P, M_TILE], f"up{group + t}", (group + t) % RING) for t in range(PACK)]
            for t in range(PACK):
                acc = accs[t]
                for a in range(K_PASSES):
                    up_pass(acc, mh, b, t, a)
                col = b * PACK + t
                nc.scalar.activation(z[:, t, :], acc[:], ACT.Relu, scale=root[:, col : col + 1])
            if mh not in h16s:
                h16s[mh] = place([P, J_PASSES, M_TILE, PACK], BF16, f"h16_{mh}", H_AT + mh * WIN_BYTES)
            split = SCALAR_COLS if group == 0 else M_TILE
            nc.scalar.activation(
                h16s[mh][:, b, :split].rearrange("p (c i) t -> p c t i", i=4),
                z[:, :, :split].rearrange("p t (c i) -> p c t i", i=4),
                ACT.Square,
            )
            if split < M_TILE:
                rest = z[:, :, split:].rearrange("p t (c i) -> p c t i", i=4)
                nc.gpsimd.tensor_tensor(
                    h16s[mh][:, b, split:].rearrange("p (c i) t -> p c t i", i=4), rest, rest, ALU.mult
                )

        def quantize_h(mh, passes, offset=None):
            if mh not in h_codes:
                h_codes[mh] = place([P, J_PASSES, M_TILE], U32, f"h_code{mh}")
            count = passes.stop - passes.start
            h_scale = place([P, count, M_TILE], U8, f"h_scale{mh}_{passes.start}", offset)
            nc.vector.quantize_mx(
                out=h_codes[mh][:, passes].rearrange("p b m -> p (b m)").bitcast(FP8X4),
                scales=h_scale[:].rearrange("p b m -> p (b m)"),
                in_=h16s[mh][:, passes].rearrange("p b m t -> p (b m t)"),
            )
            for b in range(count):
                h_scales[mh, passes.start + b] = h_scale[:, b]

        def gather_single(i, offset=None):
            pickeds[i] = place([P, 2, J_PASSES * P, 2], BF16, f"picked{i}", offset)
            nc.vector.tensor_copy(pickeds[i][:].rearrange("n u q e -> n q u e"), wd_win[i][:].indirect(offsets[:]))

        def rounded_tile(first_tile, count, offset=None):
            tile = place([P, count, J_PASSES, P, PACK], BF16, f"wd16_{first_tile}", offset)
            for e in range(count):
                wd16s[first_tile + e] = (tile, e)

        def turn_single(i, bank):
            words = pickeds[i][:].rearrange("n u q e -> n u (q e)").bitcast(F32)
            turned = bank_tile([P, 2, J_PASSES, P], f"turned{i}", bank)
            for b in range(J_PASSES):
                for u in range(2):
                    nc.tensor.transpose(turned[:, u, b, :], words[:, u, b * P : (b + 1) * P], ident[:])
            banks[i] = turned

        def sign_single(i):
            turned = banks[i]
            tile, e = wd16s[i]
            signs = sign16[:].rearrange("p b (u e) -> p b u e", e=2)
            nc.vector.tensor_tensor(
                tile[:, e].rearrange("p b n (u e) -> p b n u e", e=2),
                signs.unsqueeze(2).to_broadcast([P, J_PASSES, P, 2, 2]),
                turned[:].bitcast(BF16).rearrange("p u b (n e) -> p b n u e", e=2),
                ALU.mult,
            )

        couple_wins, banks = {}, {}

        def cast_couple(d):
            couple_wins[d] = place([P, T, 2], BF16, f"couple_win{d}", COUPLE_AT + (d - 2) * WIN_BYTES)
            for c0 in range(0, T, CAST_COLS):
                c, lo = divmod(c0, LOAD_COLS)
                nc.gpsimd.tensor_copy(
                    couple_wins[d][:, c0 : c0 + CAST_COLS, :].rearrange("p (c i) e -> p c e i", i=4),
                    raw[d, c][:, :, lo : lo + CAST_COLS].rearrange("p e (c i) -> p c e i", i=4),
                )

        def gather_couple(d, passes, first_bank, offset=None):
            count = passes.stop - passes.start
            picked = place([P, count, PACK, P], U32, f"couple_picked{d}_{passes.start}", offset)
            window = couple_wins[d][:].rearrange("p t e -> p (t e)").bitcast(U32)
            listed = offsets[:, passes.start * LIST_COLS : passes.stop * LIST_COLS]
            nc.vector.tensor_copy(picked[:].rearrange("n b t q -> n b q t"), window.indirect(listed))
            for k in range(count):
                b = passes.start + k
                turned = bank_tile([P, PACK, P], f"couple_turned{d}_{b}", first_bank + k)
                for t in range(PACK):
                    nc.tensor.transpose(turned[:, t, :], picked[:, k, t, :].bitcast(F32), ident[:])
                banks[d, b] = turned[:]

        def part_couple(d, b, halves):
            count = halves.stop - halves.start
            nc.vector.tensor_tensor(
                wd16s[2 * d][0][:, halves, b],
                sign16[:, b].unsqueeze(1).unsqueeze(1).to_broadcast([P, count, P, PACK]),
                banks[d, b].bitcast(BF16).rearrange("q t (n e) -> q e n t", e=2)[:, halves],
                ALU.mult,
            )

        def quantize_wd(first_tile, count, offset=None):
            tile, e = wd16s[first_tile]
            codes = place([P, count, J_PASSES, P], U32, f"wd_code{first_tile}")
            scales = place([P, count, J_PASSES, P], U8, f"wd_scale{first_tile}", offset)
            nc.vector.quantize_mx(
                out=codes[:].rearrange("p e b n -> p (e b n)").bitcast(FP8X4),
                scales=scales[:].rearrange("p e b n -> p (e b n)"),
                in_=tile[:, e : e + count].rearrange("p e b n t -> p (e b n t)"),
            )
            for k in range(count):
                wd_codes[first_tile + k], wd_scales[first_tile + k] = codes[:, k], scales[:, k]

        def down(i, mh, bank, offset=None, on_vector=False):
            y = bank_tile([P, M_TILE], f"down{i}_{mh}", bank)
            for b in range(J_PASSES):
                nc.tensor.matmul_mx(
                    out=y[:],
                    lhsT=wd_codes[i][:, b, :].bitcast(FP8X4),
                    lhsT_scale=wd_scales[i][:, b, :],
                    rhs=h_codes[mh][:, b].bitcast(FP8X4),
                    rhs_scale=h_scales[mh, b],
                    start=(b == 0),
                    stop=(b == J_PASSES - 1),
                )
            if offset is None:
                result = stage.tile([P, M_TILE], F32, name="result")
            else:
                result = place([P, M_TILE], F32, f"result{i}", offset)
            if on_vector:
                nc.vector.tensor_scalar(result[:], y[:], bias[:, i : i + 1], None, ALU.add)
            else:
                nc.scalar.activation(result[:], y[:], ACT.Identity, bias=bias[:, i : i + 1])
            nc.sync.dma_start(out=out_rows[i][:, mh * M_TILE : (mh + 1) * M_TILE], in_=result[:])

        both, first, second = slice(0, 2), slice(0, 1), slice(1, 2)
        rounded_tile(0, 2, WIN_BYTES)
        rounded_tile(2, 2)
        rounded_tile(4, 2)
        rounded_tile(6, 2)
        make_h(0, 0)
        for d in COUPLES:
            cast_couple(d)
        make_h(0, 1)
        make_h(1, 0)
        gather_single(0)
        gather_single(1)
        turn_single(0, 6)
        turn_single(1, 7)
        sign_single(0)
        sign_single(1)
        quantize_wd(0, 2)
        gather_single(2)
        quantize_h(0, both, 2 * WIN_BYTES)
        turn_single(2, 2)
        sign_single(2)
        make_h(1, 1)
        gather_single(3, WIN_BYTES // 2)
        quantize_h(1, first, 3 * WIN_BYTES)
        turn_single(3, 4)
        sign_single(3)
        gather_couple(2, first, 6, WIN_BYTES // 2 - 1024)
        gather_couple(2, second, 7, WIN_BYTES // 2 + 1024)
        quantize_wd(2, 2)
        part_couple(2, 0, both)
        quantize_h(1, second, WIN_BYTES // 2 + 1024)
        part_couple(2, 1, both)
        quantize_wd(4, 2, LAST_H_AT)
        for k, (i, bank) in enumerate(((0, 5), (1, 0), (2, 4), (3, 6))):
            down(i, 0, bank, Z_AT + WIN_BYTES + k * 4 * M_TILE)
        for i, bank in enumerate((1, 2, 3, 7)):
            down(i, 1, bank)
        down(4, 0, 5)
        down(4, 1, 0)
        gather_couple(3, first, 4, H_AT + WIN_BYTES)
        gather_couple(3, second, 6, H_AT + WIN_BYTES + 2048)
        down(5, 0, 1)
        part_couple(3, 0, both)
        down(5, 1, 4)
        part_couple(3, 1, first)
        quantize_wd(6, 1)
        part_couple(3, 1, second)
        quantize_wd(7, 1)
        down(6, 0, 2)
        down(6, 1, 3)
        down(7, 0, 7, on_vector=True)
        down(7, 1, 5)
